import numpy as np
import ml_dtypes


def mxq(x, axis, fmt="e4m3"):
    dtype, down = {"e4m3": (ml_dtypes.float8_e4m3fn, 7), "e5m2": (ml_dtypes.float8_e5m2, 14)}[fmt]
    v = np.moveaxis(np.asarray(x, np.float32).astype(ml_dtypes.bfloat16).astype(np.float64), axis, -1)
    blocks = v.reshape(v.shape[:-1] + (-1, 32))
    amax = np.abs(blocks).max(-1, keepdims=True)
    byte = np.maximum(np.where(amax > 0, np.frexp(amax)[1] - 1 + 127, 0) - down, 1)
    scale = np.exp2(byte - 127.0)
    codes = (blocks / scale).astype(np.float32).astype(dtype).astype(np.float64)
    return np.moveaxis((codes * scale).reshape(v.shape), -1, axis)


WIDE = False


def mx_kscale(k):
    if not WIDE:
        return np.ones(k)
    levels = np.array([30, -30])
    if k % 512:
        return np.exp2(np.random.permutation(np.resize(levels, k // 32))).repeat(32)
    a = np.empty((k // 512, 16))
    for p in range(k // 512):
        a[p, :8] = np.random.permutation(np.resize(levels, 8))
        for g in range(8):
            far = levels[np.abs(levels - a[p, g]) >= 10]
            a[p, g + 8] = far[np.random.randint(len(far))]
    return np.exp2(a.ravel()).repeat(32)


BF16 = ml_dtypes.bfloat16


def bf(x):
    return np.asarray(x, np.float32).astype(BF16)


def f64(x):
    return np.asarray(x).astype(np.float64)


M, P, F = 1024, 2048, 1024

STEP = 0.6
SPARSITY = 0.3


def soft_threshold(v, theta):
    return np.sign(v) * np.maximum(np.abs(v) - theta, 0.0)


def setup_inputs():
    s, t = mx_kscale(P), mx_kscale(F)
    return {"z": bf(np.random.standard_normal((M, P)) * s),
            "d": bf(np.random.standard_normal((P, F)) / np.sqrt(P) / s[:, None] * t),
            "x": bf(np.random.standard_normal((M, F)) * t),
            "prec": bf((1 + 0.1 * np.random.standard_normal(F)) / t ** 2),
            "eta": bf(STEP * (1 + 0.1 * np.random.standard_normal(P)) * s ** 2),
            "lam": bf(SPARSITY * (1 + 0.1 * np.random.standard_normal(P)) / s),
            "gain": bf((1 + 0.1 * np.random.standard_normal(P)) / s)}


def reference(z, d, x, prec, eta, lam, gain):
    z, d = f64(z), f64(d)
    eta = f64(eta)
    y = mxq(z, 1, "e4m3") @ mxq(d, 0, "e4m3")
    e = (y - f64(x)) * f64(prec)
    g = mxq(e, 1, "e5m2") @ mxq(d, 1, "e4m3").T
    v = z - eta * g
    return soft_threshold(v, eta * f64(lam)) * f64(gain)

@@ -1,0 +1,326 @@
+from contextlib import ExitStack
+
+import concourse.mybir as mybir
+from concourse.masks import make_identity
+
+M, P_ATOMS, F = 1024, 2048, 1024
+FLOPS = 2 * 2 * M * P_ATOMS * F
+
+F32 = mybir.dt.float32
+BF16 = mybir.dt.bfloat16
+U32 = mybir.dt.uint32
+U8 = mybir.dt.uint8
+E4M3 = mybir.dt.float8_e4m3fn_x4
+E5M2 = mybir.dt.float8_e5m2_x4
+ALU = mybir.AluOpType
+ACT = mybir.ActivationFunctionType
+
+P = 128
+W = 512
+CH = P_ATOMS // W
+FG = F // W
+HALVES = M // W
+SCALAR_IL = ((1, 1), (3, 1))
+
+
+def tile_weighted_ista_step_f3_kernel(tc, z, d, x, prec, eta, lam, gain, out):
+    nc = tc.nc
+    with ExitStack() as ctx:
+        keep = ctx.enter_context(tc.tile_pool(name="keep", bufs=1))
+        raws = ctx.enter_context(tc.tile_pool(name="raws", bufs=8))
+        bigs = ctx.enter_context(tc.tile_pool(name="bigs", bufs=4))
+        grps = ctx.enter_context(tc.tile_pool(name="grps", bufs=6))
+        xps = ctx.enter_context(tc.tile_pool(name="xps", bufs=2))
+        es = ctx.enter_context(tc.tile_pool(name="es", bufs=2))
+        vs = ctx.enter_context(tc.tile_pool(name="vs", bufs=3))
+        outs = ctx.enter_context(tc.tile_pool(name="outs", bufs=4))
+        acc = ctx.enter_context(tc.psum_pool(name="acc", bufs=4))
+        turn = ctx.enter_context(tc.psum_pool(name="turn", bufs=4))
+
+        ident = keep.tile([P, P], F32, name="ident")
+        make_identity(nc, ident[:])
+        warm = keep.tile([P, 2], F32, name="warm")
+        nc.vector.memset(warm[:], 0.0)
+        nc.scalar.activation(warm[:, 1:2], warm[:, 0:1], ACT.Copy, scale=1.0)
+
+        prec_b = keep.tile([P, FG, 4], BF16, name="prec_b")
+        eta_b = keep.tile([P, CH, 4], BF16, name="eta_b")
+        lam_b = keep.tile([P, CH, 4], BF16, name="lam_b")
+        gain_b = keep.tile([P, CH, 4], BF16, name="gain_b")
+        nc.gpsimd.dma_start(out=prec_b[:], in_=prec.rearrange("(g p t) -> p g t", p=P, t=4))
+        nc.gpsimd.dma_start(out=eta_b[:], in_=eta.rearrange("(g p t) -> p g t", p=P, t=4))
+        nc.gpsimd.dma_start(out=lam_b[:], in_=lam.rearrange("(g p t) -> p g t", p=P, t=4))
+        nc.gpsimd.dma_start(out=gain_b[:], in_=gain.rearrange("(g p t) -> p g t", p=P, t=4))
+        prec_c = keep.tile([P, FG, 4], F32, name="prec_c")
+        negeta = keep.tile([P, CH, 4], F32, name="negeta")
+        theta = keep.tile([P, CH, 4], F32, name="theta")
+        negtheta = keep.tile([P, CH, 4], F32, name="negtheta")
+        gain_c = keep.tile([P, CH, 4], F32, name="gain_c")
+        nc.gpsimd.tensor_copy(out=prec_c[:], in_=prec_b[:])
+        nc.gpsimd.tensor_scalar(negeta[:], eta_b[:], -1.0, None, ALU.mult)
+        nc.gpsimd.tensor_tensor(theta[:], eta_b[:], lam_b[:], ALU.mult)
+        nc.gpsimd.tensor_scalar(negtheta[:], theta[:], -1.0, None, ALU.mult)
+        nc.gpsimd.tensor_copy(out=gain_c[:], in_=gain_b[:])
+
+        zraw, xraw, draw = {}, {}, {}
+        zT, zc, zs = {}, {}, {}
+        dg, dc, ds = {}, {}, {}
+        tg, tcod, tsc = {}, {}, {}
+        xp, eb, eg, ec, esc = {}, {}, {}, {}, {}
+
+        def load_z(c, h):
+            t = raws.tile([P, 4, W], BF16, name="raw")
+            nc.sync.dma_start(out=t[:], in_=z[h * W:(h + 1) * W, c * W:(c + 1) * W].rearrange("(s p) k -> p s k", p=P))
+            zraw[c, h] = t
+
+        def load_x(h, fg):
+            t = raws.tile([P, 4, W], BF16, name="raw")
+            nc.sync.dma_start(out=t[:], in_=x[h * W:(h + 1) * W, fg * W:(fg + 1) * W].rearrange("(s p) k -> p s k", p=P))
+            xraw[h, fg] = t
+
+        def load_d(c):
+            t = bigs.tile([P, 4, F], BF16, name="big")
+            nc.sync.dma_start(out=t[:], in_=d[c * W:(c + 1) * W, :].rearrange("(p j) f -> p j f", j=4))
+            draw[c] = t
+
+        def z_turn(c, h):
+            words = zraw[c, h][:].bitcast(F32)
+            t = keep.tile([P, W, 4], BF16, name="zT%d%d" % (c, h), align_bytes=64)
+            zT[c, h] = t
+            dst = t[:].bitcast(F32)
+            for b in range(2):
+                bank = turn.tile([P, 2, 2, P], F32, name="bank")
+                for s in range(2):
+                    for u in range(2):
+                        nc.tensor.transpose(bank[:, u, s, :], words[:, 2 * b + s, u:256:2], ident[:])
+                nc.scalar.copy(out=dst[:, 256 * b:256 * (b + 1), :], in_=bank[:].rearrange("p u s n -> p (s n) u"))
+
+        def z_quant(c, h):
+            a = keep.tile([P, W], U32, name="zc%d%d" % (c, h), align_bytes=64)
+            b = keep.tile([P, W], U8, name="zs%d%d" % (c, h), align_bytes=64)
+            nc.vector.quantize_mx(out=a[:].bitcast(E4M3), scales=b[:], in_=zT[c, h][:].rearrange("p n t -> p (n t)"))
+            zc[c, h], zs[c, h] = a, b
+
+        def d_lay(c, fg):
+            t = grps.tile([P, W, 4], BF16, name="grp", align_bytes=64)
+            dst = t[:].rearrange("p (t m) j -> p t m j", t=4)
+            src = draw[c][:, :, fg * W:(fg + 1) * W].rearrange("p j (m t) -> p t m j", t=4)
+            if (c, fg) in SCALAR_IL:
+                nc.scalar.copy(out=dst, in_=src)
+            else:
+                nc.vector.tensor_copy(out=dst, in_=src)
+            dg[c, fg] = t
+
+        def d_quant(c, fg):
+            a = keep.tile([P, W], U32, name="dc%d%d" % (c, fg), align_bytes=64)
+            b = keep.tile([P, W], U8, name="ds%d%d" % (c, fg), align_bytes=64)
+            nc.vector.quantize_mx(out=a[:].bitcast(E4M3), scales=b[:], in_=dg[c, fg][:].rearrange("p n t -> p (n t)"))
+            dc[c, fg], ds[c, fg] = a, b
+
+        def dt_turn(c, fg):
+            words = draw[c][:].bitcast(F32)
+            t = grps.tile([P, W, 4], BF16, name="grp", align_bytes=64)
+            tg[c, fg] = t
+            dst = t[:].bitcast(F32)
+            for b in range(2):
+                bank = turn.tile([P, 2, 2, P], F32, name="bank")
+                for s in range(2):
+                    for u in range(2):
+                        nc.tensor.transpose(bank[:, u, s, :], words[:, 2 * b + s, 256 * fg + u:256 * (fg + 1):2], ident[:])
+                nc.scalar.copy(out=dst[:, 256 * b:256 * (b + 1), :], in_=bank[:].rearrange("p u s n -> p (s n) u"))
+
+        def dt_quant(c, fg):
+            a = keep.tile([P, W], U32, name="tc%d%d" % (c, fg), align_bytes=64)
+            b = keep.tile([P, W], U8, name="ts%d%d" % (c, fg), align_bytes=64)
+            nc.vector.quantize_mx(out=a[:].bitcast(E4M3), scales=b[:], in_=tg[c, fg][:].rearrange("p n t -> p (n t)"))
+            tcod[c, fg], tsc[c, fg] = a, b
+
+        def x_turn(h, fg):
+            words = xraw[h, fg][:].bitcast(F32)
+            t = xps.tile([P, 4, W], F32, name="xprec")
+            xp[h, fg] = t
+            for u in range(2):
+                bank = turn.tile([P, 4, P], F32, name="bank")
+                for s in range(4):
+                    nc.tensor.transpose(bank[:, s, :], words[:, s, u:256:2], ident[:])
+                pairs = bank[:].rearrange("p s n -> p (s n)").bitcast(BF16).rearrange("p (n e) -> p n e", e=2)
+                for e in range(2):
+                    k = 2 * u + e
+                    nc.scalar.activation(t[:, k, :], pairs[:, :, e], ACT.Copy, scale=prec_c[:, fg, k:k + 1])
+
+        def s1_pass(y, h, fg, t, c):
+            nc.tensor.matmul_mx(
+                out=y[:],
+                lhsT=dc[c, fg][:, t * P:(t + 1) * P].bitcast(E4M3),
+                lhsT_scale=ds[c, fg][:, t * P:(t + 1) * P],
+                rhs=zc[c, h][:].bitcast(E4M3),
+                rhs_scale=zs[c, h][:],
+                start=(c == 0),
+                stop=(c == CH - 1),
+            )
+
+        def residual(y, h, fg, t):
+            if t == 0:
+                eb[h, fg] = es.tile([P, 4, W], BF16, name="ebf")
+            nc.vector.scalar_tensor_tensor(
+                out=eb[h, fg][:, t, :], in0=y[:], scalar=prec_c[:, fg, t:t + 1], in1=xp[h, fg][:, t, :],
+                op0=ALU.mult, op1=ALU.subtract)
+
+        def e_lay(h, fg, engine):
+            t = grps.tile([P, W, 4], BF16, name="grp", align_bytes=64)
+            src = eb[h, fg][:].rearrange("p t n -> p n t")
+            if engine == "scalar":
+                nc.scalar.copy(out=t[:], in_=src)
+            else:
+                nc.vector.tensor_copy(out=t[:], in_=src)
+            eg[h, fg] = t
+
+        def e_quant(h, fg):
+            a = keep.tile([P, W], U32, name="ec%d%d" % (h, fg), align_bytes=64)
+            b = keep.tile([P, W], U8, name="ec_s%d%d" % (h, fg), align_bytes=64)
+            nc.vector.quantize_mx(out=a[:].bitcast(E5M2), scales=b[:], in_=eg[h, fg][:].rearrange("p n t -> p (n t)"))
+            ec[h, fg], esc[h, fg] = a, b
+
+        def stage1(h, fg):
+            for t in range(4):
+                y = acc.tile([P, W], F32, name="sums")
+                for c in range(CH):
+                    s1_pass(y, h, fg, t, c)
+                residual(y, h, fg, t)
+
+        def stage2(g, h):
+            hi = bigs.tile([P, 4, W], F32, name="big")
+            lo = bigs.tile([P, 4, W], F32, name="big")
+            waiting = []
+
+            def shrink(j, v):
+                nc.vector.tensor_scalar(hi[:, j, :], v[:], theta[:, g, j:j + 1], gain_c[:, g, j:j + 1], ALU.max, ALU.mult)
+                nc.vector.tensor_scalar(lo[:, j, :], v[:], negtheta[:, g, j:j + 1], gain_c[:, g, j:j + 1], ALU.min, ALU.mult)
+
+            for j in range(4):
+                y = acc.tile([P, W], F32, name="sums")
+                for fg in range(FG):
+                    nc.tensor.matmul_mx(
+                        out=y[:],
+                        lhsT=tcod[g, fg][:, j * P:(j + 1) * P].bitcast(E4M3),
+                        lhsT_scale=tsc[g, fg][:, j * P:(j + 1) * P],
+                        rhs=ec[h, fg][:].bitcast(E5M2),
+                        rhs_scale=esc[h, fg][:],
+                        start=(fg == 0),
+                        stop=(fg == FG - 1),
+                    )
+                v = vs.tile([P, W], F32, name="v")
+                nc.vector.scalar_tensor_tensor(
+                    out=v[:], in0=y[:], scalar=negeta[:, g, j:j + 1], in1=zT[g, h][:, :, j],
+                    op0=ALU.mult, op1=ALU.add)
+                waiting.append((j, v))
+                if len(waiting) == 2:
+                    shrink(*waiting[0])
+                    waiting = waiting[1:]
+            shrink(*waiting[0])
+            return hi, lo
+
+        def turn_pair(bank, j, s, hi, lo):
+            cols = slice(s * P, (s + 1) * P)
+            nc.tensor.matmul(bank[:, j, :], lhsT=hi[:, j, cols], rhs=ident[:], is_transpose=True, start=True, stop=False)
+            nc.tensor.matmul(bank[:, j, :], lhsT=lo[:, j, cols], rhs=ident[:], is_transpose=True, start=False, stop=True)
+
+        def leave(bank, g, h, s, engine):
+            o = outs.tile([P, W], F32, name="o")
+            src = bank[:].rearrange("p j n -> p n j")
+            dst = o[:].rearrange("p (n j) -> p n j", j=4)
+            if engine == "scalar":
+                nc.scalar.copy(out=dst, in_=src)
+            else:
+                nc.vector.tensor_copy(out=dst, in_=src)
+            r = h * W + s * P
+            nc.sync.dma_start(out=out[r:r + P, g * W:(g + 1) * W], in_=o[:])
+
+        def finish(g, h, hi, lo, last):
+            if last:
+                banks = []
+                for s in range(4):
+                    bank = turn.tile([P, 4, P], F32, name="bank")
+                    banks.append(bank)
+                for j in range(4):
+                    for s in range(4):
+                        turn_pair(banks[s], j, s, hi, lo)
+                for s in range(4):
+                    leave(banks[s], g, h, s, "scalar" if s % 2 == 0 else "vector")
+            else:
+                for s in range(4):
+                    bank = turn.tile([P, 4, P], F32, name="bank")
+                    for j in range(4):
+                        turn_pair(bank, j, s, hi, lo)
+                    leave(bank, g, h, s, "scalar")
+
+        ctx.enter_context(tc.manual_schedule())
+
+        for c in range(CH):
+            load_z(c, 0)
+            if c == 3:
+                load_x(0, 0)
+            load_d(c)
+        load_x(0, 1)
+
+        first = []
+        for c in range(CH):
+            z_turn(c, 0)
+            d_lay(c, 0)
+            d_lay(c, 1)
+            z_quant(c, 0)
+            d_quant(c, 0)
+            dt_turn(c, 0)
+            d_quant(c, 1)
+            dt_turn(c, 1)
+            if c == 3:
+                x_turn(0, 0)
+            if c > 0:
+                dt_quant(c - 1, 0)
+                dt_quant(c - 1, 1)
+            for t in range(4):
+                if c == 0:
+                    y = acc.tile([P, W], F32, name="sums")
+                    first.append(y)
+                s1_pass(first[t], 0, 0, t, c)
+
+        for c in range(CH):
+            load_z(c, 1)
+        load_x(1, 0)
+        load_x(1, 1)
+
+        x_turn(0, 1)
+        for t in range(4):
+            residual(first[t], 0, 0, t)
+        e_lay(0, 0, "scalar")
+        stage1(0, 1)
+        dt_quant(3, 0)
+        e_quant(0, 0)
+        for c in range(CH):
+            z_turn(c, 1)
+            if c == 0:
+                e_lay(0, 1, "vector")
+                dt_quant(3, 1)
+                e_quant(0, 1)
+            z_quant(c, 1)
+        x_turn(1, 0)
+        stage1(1, 0)
+        x_turn(1, 1)
+        e_lay(1, 0, "scalar")
+        stage1(1, 1)
+        e_quant(1, 0)
+        e_lay(1, 1, "vector")
+
+        groups = []
+        for h in range(HALVES):
+            for g in range(CH):
+                groups.append((g, h))
+        before = None
+        for n, (g, h) in enumerate(groups):
+            if n == 2:
+                e_quant(1, 1)
+            hi, lo = stage2(g, h)
+            if before is not None:
+                finish(*before, False)
+            before = (g, h, hi, lo)
+        finish(*before, True)

@@ -20,19 +20,31 @@ W = 512
 CH = P_ATOMS // W
 FG = F // W
 HALVES = M // W
-SCALAR_IL = ((1, 1), (3, 1))
+SCALAR_IL = ((2, 1), (3, 1))
+WARM0 = 6
+WARM = (2, 2, 1, 1)
+HEAD = (((0, 0),), ((0, 1),), ((1, 0),))
+SLOTS = (("z", 0, 1), ("z", 1, 1), ("z", 2, 1), ("z", 3, 1), ("x", 1, 1), ("d", 1, 1), ("d", 2, 0), ("d", 2, 1), ("d", 3, 0), ("d", 3, 1))
+EXTRA = ("x", 1, 0)
+LAY = ("scalar", "vector", "scalar", "vector")
+SPLIT = False
+KINDS = ("ZKZK",) * 7 + ("ZDZD",)
+LATE = ((),)
+LAYW = True
+LAG = 2
+OUT = ("scalar", "scalar", "scalar", "vector")
 
 
 def tile_weighted_ista_step_f3_kernel(tc, z, d, x, prec, eta, lam, gain, out):
     nc = tc.nc
     with ExitStack() as ctx:
         keep = ctx.enter_context(tc.tile_pool(name="keep", bufs=1))
-        raws = ctx.enter_context(tc.tile_pool(name="raws", bufs=8))
-        bigs = ctx.enter_context(tc.tile_pool(name="bigs", bufs=4))
+        raws = ctx.enter_context(tc.tile_pool(name="raws", bufs=11))
+        bigs = ctx.enter_context(tc.tile_pool(name="bigs", bufs=5))
         grps = ctx.enter_context(tc.tile_pool(name="grps", bufs=6))
-        xps = ctx.enter_context(tc.tile_pool(name="xps", bufs=2))
+        zcs = ctx.enter_context(tc.tile_pool(name="zcs", bufs=4))
         es = ctx.enter_context(tc.tile_pool(name="es", bufs=2))
-        vs = ctx.enter_context(tc.tile_pool(name="vs", bufs=3))
+        vs = ctx.enter_context(tc.tile_pool(name="vs", bufs=8))
         outs = ctx.enter_context(tc.tile_pool(name="outs", bufs=4))
         acc = ctx.enter_context(tc.psum_pool(name="acc", bufs=4))
         turn = ctx.enter_context(tc.psum_pool(name="turn", bufs=4))
@@ -43,24 +55,53 @@ def tile_weighted_ista_step_f3_kernel(tc, z, d, x, prec, eta, lam, gain, out):
         nc.vector.memset(warm[:], 0.0)
         nc.scalar.activation(warm[:, 1:2], warm[:, 0:1], ACT.Copy, scale=1.0)
 
-        prec_b = keep.tile([P, FG, 4], BF16, name="prec_b")
-        eta_b = keep.tile([P, CH, 4], BF16, name="eta_b")
-        lam_b = keep.tile([P, CH, 4], BF16, name="lam_b")
-        gain_b = keep.tile([P, CH, 4], BF16, name="gain_b")
-        nc.gpsimd.dma_start(out=prec_b[:], in_=prec.rearrange("(g p t) -> p g t", p=P, t=4))
-        nc.gpsimd.dma_start(out=eta_b[:], in_=eta.rearrange("(g p t) -> p g t", p=P, t=4))
-        nc.gpsimd.dma_start(out=lam_b[:], in_=lam.rearrange("(g p t) -> p g t", p=P, t=4))
-        nc.gpsimd.dma_start(out=gain_b[:], in_=gain.rearrange("(g p t) -> p g t", p=P, t=4))
-        prec_c = keep.tile([P, FG, 4], F32, name="prec_c")
-        negeta = keep.tile([P, CH, 4], F32, name="negeta")
-        theta = keep.tile([P, CH, 4], F32, name="theta")
-        negtheta = keep.tile([P, CH, 4], F32, name="negtheta")
-        gain_c = keep.tile([P, CH, 4], F32, name="gain_c")
-        nc.gpsimd.tensor_copy(out=prec_c[:], in_=prec_b[:])
-        nc.gpsimd.tensor_scalar(negeta[:], eta_b[:], -1.0, None, ALU.mult)
-        nc.gpsimd.tensor_tensor(theta[:], eta_b[:], lam_b[:], ALU.mult)
-        nc.gpsimd.tensor_scalar(negtheta[:], theta[:], -1.0, None, ALU.mult)
-        nc.gpsimd.tensor_copy(out=gain_c[:], in_=gain_b[:])
+        ctx.enter_context(tc.manual_schedule())
+
+        consts = {}
+        rows = keep.tile([P, W], BF16, name="rows", align_bytes=64)
+        blank = keep.tile([P, W], BF16, name="blank")
+        nc.vector.memset(blank[:], 0.0)
+        nc.vector.memset(rows[:], 0.0)
+
+        def warm_up(n):
+            bank = turn.tile([P, W], F32, name="bank")
+            for k in range(n):
+                nc.tensor.matmul(bank[:], lhsT=blank[:, 0:P], rhs=blank[:], start=True, stop=True)
+
+        def load_rows():
+            for r, src in ((0, prec), (32, eta), (64, lam), (96, gain)):
+                v = src.rearrange("(g k) -> g k", k=W)
+                nc.sync.dma_start(out=rows[r:r + v.shape[0], :], in_=v)
+
+        def make_consts():
+            words = rows[:].bitcast(F32)
+            bank = turn.tile([P, 4, P], F32, name="bank")
+            for u in range(2):
+                nc.tensor.transpose(bank[:, u, :], words[:, u:256:2], ident[:])
+            table = keep.tile([P, 100, 4], F32, name="table")
+            for u in range(2):
+                pairs = bank[:, u, :].bitcast(BF16).rearrange("p (r e) -> p r e", e=2)
+                nc.vector.tensor_copy(out=table[:, :, 2 * u:2 * u + 2], in_=pairs[:, 0:100, :])
+            c = consts
+            c["prec"] = table[:, 0:2, :]
+            c["eta"] = table[:, 32:36, :]
+            c["lam"] = table[:, 64:68, :]
+            c["gain"] = table[:, 96:100, :]
+            for name in ("neta", "th", "nth", "ngeta", "gth", "ngth", "ngain"):
+                t = keep.tile([P, CH, 4], F32, name=name + "_c")
+                c[name] = t[:]
+            g = nc.gpsimd
+            g.tensor_scalar(c["neta"], c["eta"], -1.0, None, ALU.mult)
+            g.tensor_tensor(c["th"], c["eta"], c["lam"], ALU.mult)
+            g.tensor_scalar(c["nth"], c["th"], -1.0, None, ALU.mult)
+            g.tensor_tensor(c["ngeta"], c["neta"], c["gain"], ALU.mult)
+
+        def gain_thresholds():
+            c = consts
+            t = keep.tile([P, CH, 4], F32, name="absg")
+            nc.vector.scalar_tensor_tensor(out=t[:], in0=c["gain"], scalar=-1.0, in1=c["gain"], op0=ALU.mult, op1=ALU.max)
+            nc.vector.tensor_tensor(c["gth"], t[:], c["th"], ALU.mult)
+            nc.vector.tensor_scalar(c["ngth"], c["gth"], -1.0, None, ALU.mult)
 
         zraw, xraw, draw = {}, {}, {}
         zT, zc, zs = {}, {}, {}
@@ -83,6 +124,24 @@ def tile_weighted_ista_step_f3_kernel(tc, z, d, x, prec, eta, lam, gain, out):
             nc.sync.dma_start(out=t[:], in_=d[c * W:(c + 1) * W, :].rearrange("(p j) f -> p j f", j=4))
             draw[c] = t
 
+        laid = {}
+
+        def lay_words(kind, a, b):
+            if kind == "d":
+                src = draw[a][:].bitcast(F32)[:, :, 256 * b:256 * (b + 1)]
+            elif kind == "z":
+                src = zraw[a, b][:].bitcast(F32)
+            else:
+                src = xraw[a, b][:].bitcast(F32)
+            t = raws.tile([P, 4, 2, P], F32, name="raw")
+            nc.vector.tensor_copy(out=t[:], in_=src.rearrange("p s (w u) -> p s u w", u=2))
+            laid[kind, a, b] = t
+
+        def words_of(kind, a, b, src, s, u):
+            if (kind, a, b) in laid:
+                return laid[kind, a, b][:, s, u, :]
+            return src[:, s, u:256:2]
+
         def z_turn(c, h):
             words = zraw[c, h][:].bitcast(F32)
             t = keep.tile([P, W, 4], BF16, name="zT%d%d" % (c, h), align_bytes=64)
@@ -92,12 +151,12 @@ def tile_weighted_ista_step_f3_kernel(tc, z, d, x, prec, eta, lam, gain, out):
                 bank = turn.tile([P, 2, 2, P], F32, name="bank")
                 for s in range(2):
                     for u in range(2):
-                        nc.tensor.transpose(bank[:, u, s, :], words[:, 2 * b + s, u:256:2], ident[:])
+                        nc.tensor.transpose(bank[:, u, s, :], words_of("z", c, h, words, 2 * b + s, u), ident[:])
                 nc.scalar.copy(out=dst[:, 256 * b:256 * (b + 1), :], in_=bank[:].rearrange("p u s n -> p (s n) u"))
 
         def z_quant(c, h):
-            a = keep.tile([P, W], U32, name="zc%d%d" % (c, h), align_bytes=64)
-            b = keep.tile([P, W], U8, name="zs%d%d" % (c, h), align_bytes=64)
+            a = zcs.tile([P, W], U32, name="zcode", align_bytes=64)
+            b = zcs.tile([P, W], U8, name="zscale", align_bytes=64)
             nc.vector.quantize_mx(out=a[:].bitcast(E4M3), scales=b[:], in_=zT[c, h][:].rearrange("p n t -> p (n t)"))
             zc[c, h], zs[c, h] = a, b
 
@@ -118,7 +177,7 @@ def tile_weighted_ista_step_f3_kernel(tc, z, d, x, prec, eta, lam, gain, out):
             dc[c, fg], ds[c, fg] = a, b
 
         def dt_turn(c, fg):
-            words = draw[c][:].bitcast(F32)
+            words = draw[c][:].bitcast(F32)[:, :, 256 * fg:256 * (fg + 1)]
             t = grps.tile([P, W, 4], BF16, name="grp", align_bytes=64)
             tg[c, fg] = t
             dst = t[:].bitcast(F32)
@@ -126,7 +185,7 @@ def tile_weighted_ista_step_f3_kernel(tc, z, d, x, prec, eta, lam, gain, out):
                 bank = turn.tile([P, 2, 2, P], F32, name="bank")
                 for s in range(2):
                     for u in range(2):
-                        nc.tensor.transpose(bank[:, u, s, :], words[:, 2 * b + s, 256 * fg + u:256 * (fg + 1):2], ident[:])
+                        nc.tensor.transpose(bank[:, u, s, :], words_of("d", c, fg, words, 2 * b + s, u), ident[:])
                 nc.scalar.copy(out=dst[:, 256 * b:256 * (b + 1), :], in_=bank[:].rearrange("p u s n -> p (s n) u"))
 
         def dt_quant(c, fg):
@@ -137,16 +196,16 @@ def tile_weighted_ista_step_f3_kernel(tc, z, d, x, prec, eta, lam, gain, out):
 
         def x_turn(h, fg):
             words = xraw[h, fg][:].bitcast(F32)
-            t = xps.tile([P, 4, W], F32, name="xprec")
+            t = bigs.tile([P, 4, W], F32, name="big")
             xp[h, fg] = t
             for u in range(2):
                 bank = turn.tile([P, 4, P], F32, name="bank")
                 for s in range(4):
-                    nc.tensor.transpose(bank[:, s, :], words[:, s, u:256:2], ident[:])
+                    nc.tensor.transpose(bank[:, s, :], words_of("x", h, fg, words, s, u), ident[:])
                 pairs = bank[:].rearrange("p s n -> p (s n)").bitcast(BF16).rearrange("p (n e) -> p n e", e=2)
                 for e in range(2):
                     k = 2 * u + e
-                    nc.scalar.activation(t[:, k, :], pairs[:, :, e], ACT.Copy, scale=prec_c[:, fg, k:k + 1])
+                    nc.scalar.activation(t[:, k, :], pairs[:, :, e], ACT.Copy, scale=consts["prec"][:, fg, k:k + 1])
 
         def s1_pass(y, h, fg, t, c):
             nc.tensor.matmul_mx(
@@ -163,7 +222,7 @@ def tile_weighted_ista_step_f3_kernel(tc, z, d, x, prec, eta, lam, gain, out):
             if t == 0:
                 eb[h, fg] = es.tile([P, 4, W], BF16, name="ebf")
             nc.vector.scalar_tensor_tensor(
-                out=eb[h, fg][:, t, :], in0=y[:], scalar=prec_c[:, fg, t:t + 1], in1=xp[h, fg][:, t, :],
+                out=eb[h, fg][:, t, :], in0=y[:], scalar=consts["prec"][:, fg, t:t + 1], in1=xp[h, fg][:, t, :],
                 op0=ALU.mult, op1=ALU.subtract)
 
         def e_lay(h, fg, engine):
@@ -181,51 +240,89 @@ def tile_weighted_ista_step_f3_kernel(tc, z, d, x, prec, eta, lam, gain, out):
             nc.vector.quantize_mx(out=a[:].bitcast(E5M2), scales=b[:], in_=eg[h, fg][:].rearrange("p n t -> p (n t)"))
             ec[h, fg], esc[h, fg] = a, b
 
-        def stage1(h, fg):
-            for t in range(4):
-                y = acc.tile([P, W], F32, name="sums")
-                for c in range(CH):
-                    s1_pass(y, h, fg, t, c)
-                residual(y, h, fg, t)
+        def s1_unit(h, fg, t):
+            y = acc.tile([P, W], F32, name="sums")
+            for c in range(CH):
+                s1_pass(y, h, fg, t, c)
+            residual(y, h, fg, t)
 
-        def stage2(g, h):
-            hi = bigs.tile([P, 4, W], F32, name="big")
-            lo = bigs.tile([P, 4, W], F32, name="big")
-            waiting = []
+        leaf = {}
+        pend = {}
 
-            def shrink(j, v):
-                nc.vector.tensor_scalar(hi[:, j, :], v[:], theta[:, g, j:j + 1], gain_c[:, g, j:j + 1], ALU.max, ALU.mult)
-                nc.vector.tensor_scalar(lo[:, j, :], v[:], negtheta[:, g, j:j + 1], gain_c[:, g, j:j + 1], ALU.min, ALU.mult)
+        def s2_sums(g, h, j):
+            y = acc.tile([P, W], F32, name="sums")
+            for fg in range(FG):
+                nc.tensor.matmul_mx(
+                    out=y[:],
+                    lhsT=tcod[g, fg][:, j * P:(j + 1) * P].bitcast(E4M3),
+                    lhsT_scale=tsc[g, fg][:, j * P:(j + 1) * P],
+                    rhs=ec[h, fg][:].bitcast(E5M2),
+                    rhs_scale=esc[h, fg][:],
+                    start=(fg == 0),
+                    stop=(fg == FG - 1),
+                )
+            return y
 
-            for j in range(4):
-                y = acc.tile([P, W], F32, name="sums")
-                for fg in range(FG):
-                    nc.tensor.matmul_mx(
-                        out=y[:],
-                        lhsT=tcod[g, fg][:, j * P:(j + 1) * P].bitcast(E4M3),
-                        lhsT_scale=tsc[g, fg][:, j * P:(j + 1) * P],
-                        rhs=ec[h, fg][:].bitcast(E5M2),
-                        rhs_scale=esc[h, fg][:],
-                        start=(fg == 0),
-                        stop=(fg == FG - 1),
-                    )
+        def col(name, g, j):
+            return consts[name][:, g, j:j + 1]
+
+        def step_plain(y, g, h, j):
+            v = vs.tile([P, W], F32, name="v")
+            nc.vector.scalar_tensor_tensor(
+                out=v[:], in0=y[:], scalar=col("neta", g, j), in1=zT[g, h][:, :, j], op0=ALU.mult, op1=ALU.add)
+            pend[g, h, j] = v
+
+        def split_plain(g, h, j):
+            v = pend[g, h, j]
+            t = raws.tile([P, 2, W], F32, name="raw")
+            nc.vector.tensor_scalar(t[:, 0, :], v[:], col("th", g, j), col("gain", g, j), ALU.max, ALU.mult)
+            nc.vector.tensor_scalar(t[:, 1, :], v[:], col("nth", g, j), col("gain", g, j), ALU.min, ALU.mult)
+            leaf[g, h, j] = (t[:, 0, :], t[:, 1, :])
+
+        made = {}
+
+        def gain_z(g, h, j):
+            if KINDS[CH * h + g][j] == "K":
+                t = raws.tile([P, 2, W], F32, name="raw")
+                made[g, h, j] = t
+                dst = t[:, 0, :]
+            else:
                 v = vs.tile([P, W], F32, name="v")
-                nc.vector.scalar_tensor_tensor(
-                    out=v[:], in0=y[:], scalar=negeta[:, g, j:j + 1], in1=zT[g, h][:, :, j],
-                    op0=ALU.mult, op1=ALU.add)
-                waiting.append((j, v))
-                if len(waiting) == 2:
-                    shrink(*waiting[0])
-                    waiting = waiting[1:]
-            shrink(*waiting[0])
-            return hi, lo
+                dst = v[:]
+            pend[g, h, j] = dst
+            nc.gpsimd.tensor_scalar(dst, zT[g, h][:, :, j], col("gain", g, j), 0.0, ALU.mult, ALU.add)
 
-        def turn_pair(bank, j, s, hi, lo):
+        def step_gained(y, g, h, j):
+            v = pend[g, h, j]
+            nc.vector.scalar_tensor_tensor(
+                out=v, in0=y[:], scalar=col("ngeta", g, j), in1=v, op0=ALU.mult, op1=ALU.add)
+            if KINDS[CH * h + g][j] == "K":
+                c = made[g, h, j][:, 1, :]
+                nc.scalar.activation(c, v, ACT.Copy, scale=-1.0)
+                leaf[g, h, j] = (v, c)
+            else:
+                r = vs.tile([P, W], F32, name="v")
+                nc.scalar.activation(r[:], v, ACT.Relu, bias=col("ngth", g, j))
+                pend[g, h, j] = (v, r)
+
+        def clamp(g, h, j):
+            c = leaf[g, h, j][1]
+            nc.gpsimd.tensor_scalar(c, c, col("gth", g, j), col("ngth", g, j), ALU.min, ALU.max)
+
+        def join_gained(g, h, j, dst):
+            v, r = pend[g, h, j]
+            nc.vector.scalar_tensor_tensor(
+                out=dst, in0=v, scalar=col("gth", g, j), in1=r[:], op0=ALU.add, op1=ALU.min)
+            leaf[g, h, j] = (dst,)
+
+        def turn_out(g, h, s, engine):
+            bank = turn.tile([P, 4, P], F32, name="bank")
             cols = slice(s * P, (s + 1) * P)
-            nc.tensor.matmul(bank[:, j, :], lhsT=hi[:, j, cols], rhs=ident[:], is_transpose=True, start=True, stop=False)
-            nc.tensor.matmul(bank[:, j, :], lhsT=lo[:, j, cols], rhs=ident[:], is_transpose=True, start=False, stop=True)
-
-        def leave(bank, g, h, s, engine):
+            for j in range(4):
+                parts = leaf[g, h, j]
+                for k in range(len(parts)):
+                    nc.tensor.matmul(bank[:, j, :], lhsT=parts[k][:, cols], rhs=ident[:], is_transpose=True,
+                                     start=(k == 0), stop=(k == len(parts) - 1))
             o = outs.tile([P, W], F32, name="o")
             src = bank[:].rearrange("p j n -> p n j")
             dst = o[:].rearrange("p (n j) -> p n j", j=4)
@@ -236,91 +333,166 @@ def tile_weighted_ista_step_f3_kernel(tc, z, d, x, prec, eta, lam, gain, out):
             r = h * W + s * P
             nc.sync.dma_start(out=out[r:r + P, g * W:(g + 1) * W], in_=o[:])
 
-        def finish(g, h, hi, lo, last):
-            if last:
-                banks = []
-                for s in range(4):
-                    bank = turn.tile([P, 4, P], F32, name="bank")
-                    banks.append(bank)
+        def nothing():
+            return None
+
+        def gain_ahead(n):
+            if n < 8:
+                g, h = order[n]
                 for j in range(4):
-                    for s in range(4):
-                        turn_pair(banks[s], j, s, hi, lo)
-                for s in range(4):
-                    leave(banks[s], g, h, s, "scalar" if s % 2 == 0 else "vector")
+                    if KINDS[n][j] in "ZK":
+                        gain_z(g, h, j)
+
+        def finish_unit(n, j, pair):
+            g, h = order[n]
+            k = KINDS[n][j]
+            if k == "D":
+                split_plain(g, h, j)
+            elif k == "K":
+                clamp(g, h, j)
             else:
-                for s in range(4):
-                    bank = turn.tile([P, 4, P], F32, name="bank")
-                    for j in range(4):
-                        turn_pair(bank, j, s, hi, lo)
-                    leave(bank, g, h, s, "scalar")
+                join_gained(g, h, j, pair[:, j // 2, :])
 
-        ctx.enter_context(tc.manual_schedule())
+        def group(n, between, after):
+            g, h = order[n]
+            kinds = KINDS[n]
+            pair = None
+            if "Z" in kinds:
+                pair = raws.tile([P, 2, W], F32, name="raw")
+            gain_ahead(n + 1)
+            for j in range(4):
+                y = s2_sums(g, h, j)
+                if kinds[j] == "D":
+                    step_plain(y, g, h, j)
+                else:
+                    step_gained(y, g, h, j)
+                if j == 1:
+                    between()
+                if j >= LAG:
+                    finish_unit(n, j - LAG, pair)
+            for j in range(4 - LAG, 4):
+                finish_unit(n, j, pair)
+            after()
 
-        for c in range(CH):
-            load_z(c, 0)
-            if c == 3:
-                load_x(0, 0)
-            load_d(c)
+        load_z(0, 0)
+        load_rows()
+        load_d(0)
+        load_z(1, 0)
+        load_d(1)
+        load_z(2, 0)
+        load_d(2)
+        load_z(3, 0)
+        load_d(3)
+        load_x(0, 0)
         load_x(0, 1)
-
-        first = []
-        for c in range(CH):
-            z_turn(c, 0)
-            d_lay(c, 0)
-            d_lay(c, 1)
-            z_quant(c, 0)
-            d_quant(c, 0)
-            dt_turn(c, 0)
-            d_quant(c, 1)
-            dt_turn(c, 1)
-            if c == 3:
-                x_turn(0, 0)
-            if c > 0:
-                dt_quant(c - 1, 0)
-                dt_quant(c - 1, 1)
-            for t in range(4):
-                if c == 0:
-                    y = acc.tile([P, W], F32, name="sums")
-                    first.append(y)
-                s1_pass(first[t], 0, 0, t, c)
-
         for c in range(CH):
             load_z(c, 1)
         load_x(1, 0)
         load_x(1, 1)
 
-        x_turn(0, 1)
-        for t in range(4):
-            residual(first[t], 0, 0, t)
-        e_lay(0, 0, "scalar")
-        stage1(0, 1)
-        dt_quant(3, 0)
-        e_quant(0, 0)
-        for c in range(CH):
-            z_turn(c, 1)
-            if c == 0:
-                e_lay(0, 1, "vector")
-                dt_quant(3, 1)
-                e_quant(0, 1)
-            z_quant(c, 1)
-        x_turn(1, 0)
-        stage1(1, 0)
-        x_turn(1, 1)
-        e_lay(1, 0, "scalar")
-        stage1(1, 1)
-        e_quant(1, 0)
-        e_lay(1, 1, "vector")
+        def sums():
+            y = acc.tile([P, W], F32, name="sums")
+            return y
 
-        groups = []
-        for h in range(HALVES):
-            for g in range(CH):
-                groups.append((g, h))
-        before = None
-        for n, (g, h) in enumerate(groups):
+        order = [(g, h) for h in range(HALVES) for g in range(CH)]
+        turns = {"z": z_turn, "d": dt_turn, "x": x_turn}
+
+        def turn_in(f):
+            turns[f[0]](f[1], f[2])
+
+        def lay(f):
+            if LAYW:
+                lay_words(*f)
+
+        first = []
+        for t in range(4):
+            first.append(sums())
+        warm_up(WARM0)
+        make_consts()
+        for c in range(CH):
+            z_turn(c, 0)
+            warm_up(WARM[c])
+            d_lay(c, 0)
+            z_quant(c, 0)
+            d_quant(c, 0)
+            d_lay(c, 1)
+            if c > 0:
+                for t in range(4):
+                    s1_pass(first[t], 0, 0, t, c - 1)
+                for f in HEAD[c - 1]:
+                    dt_turn(*f)
+            d_quant(c, 1)
+            if c > 1:
+                for f in HEAD[c - 2]:
+                    dt_quant(*f)
+        x_turn(0, 0)
+        lay(SLOTS[0])
+        for t in range(4):
+            s1_pass(first[t], 0, 0, t, 3)
+            residual(first[t], 0, 0, t)
+        x_turn(0, 1)
+        for f in HEAD[2]:
+            dt_quant(*f)
+        for n in range(12):
+            h, fg, t = ((0, 1), (1, 0), (1, 1))[n // 4] + (n % 4,)
+            if n + 1 < len(SLOTS):
+                lay(SLOTS[n + 1])
+            s1_unit(h, fg, t)
+            if n < len(SLOTS):
+                turn_in(SLOTS[n])
+            if n == 3:
+                turn_in(EXTRA)
+            if 0 < n <= len(SLOTS):
+                f = SLOTS[n - 1]
+                if f[0] == "z" and f[1] < 3:
+                    z_quant(f[1], f[2])
+                elif f[0] == "d":
+                    dt_quant(f[1], f[2])
+            if n == 3:
+                z_quant(3, 1)
+            if n == 0:
+                e_lay(0, 0, LAY[0])
             if n == 2:
-                e_quant(1, 1)
-            hi, lo = stage2(g, h)
-            if before is not None:
-                finish(*before, False)
-            before = (g, h, hi, lo)
-        finish(*before, True)
+                e_quant(0, 0)
+            if n == 4:
+                e_lay(0, 1, LAY[1])
+            if n == 6:
+                e_quant(0, 1)
+            if n == 8:
+                e_lay(1, 0, LAY[2])
+                gain_thresholds()
+            if n == 10:
+                e_quant(1, 0)
+                gain_ahead(0)
+
+        for f in LATE[0]:
+            lay(f)
+        for n in range(8):
+            def between(n=n):
+                if SPLIT and n > 1:
+                    for s in (2, 3):
+                        turn_out(*order[n - 2], s, "scalar")
+                if n < len(LATE):
+                    for f in LATE[n]:
+                        turn_in(f)
+                if 0 < n <= len(LATE):
+                    for f in LATE[n - 1]:
+                        dt_quant(f[1], f[2])
+                if n == 1:
+                    e_lay(1, 1, LAY[3])
+                if n == 2:
+                    e_quant(1, 1)
+
+            def after(n=n):
+                if n > 0:
+                    for s in (0, 1) if SPLIT else range(4):
+                        turn_out(*order[n - 1], s, OUT[s])
+            if 0 < n < len(LATE):
+                for f in LATE[n]:
+                    lay(f)
+            group(n, between, after)
+        if SPLIT:
+            for s in (2, 3):
+                turn_out(*order[6], s, "scalar")
+        for s in range(4):
+            turn_out(*order[7], s, "scalar" if s % 2 == 0 else "vector")

@@ -20,19 +20,19 @@ W = 512
 CH = P_ATOMS // W
 FG = F // W
 HALVES = M // W
-SCALAR_IL = ((2, 1), (3, 1))
+SCALAR_IL = ((1, 1), (2, 1), (3, 1))
 WARM0 = 6
 WARM = (2, 2, 1, 1)
-HEAD = (((0, 0),), ((0, 1),), ((1, 0),))
-SLOTS = (("z", 0, 1), ("z", 1, 1), ("z", 2, 1), ("z", 3, 1), ("x", 1, 1), ("d", 1, 1), ("d", 2, 0), ("d", 2, 1), ("d", 3, 0), ("d", 3, 1))
-EXTRA = ("x", 1, 0)
-LAY = ("scalar", "vector", "scalar", "vector")
-SPLIT = False
-KINDS = ("ZKZK",) * 7 + ("ZDZD",)
-LATE = ((),)
-LAYW = True
+KINDS = ("DDDD",) * 8
+SCALAR_WORDS = (("z", 0, 1), ("z", 1, 1), ("z", 2, 1), ("z", 3, 1), ("d", 1, 1), ("d", 2, 0), ("d", 2, 1), ("d", 3, 0), ("d", 3, 1))
+FAST = True
 LAG = 2
-OUT = ("scalar", "scalar", "scalar", "vector")
+OUT = ("scalar",) * 4
+LOADS = "z00 r d0 z10 d1 z20 d2 x00 z30 d3 x01 z01 z11 z21 z31 x10 x11"
+HEAD = ((("d", 0, 0),), (("d", 0, 1),), (("d", 1, 0),))
+SLOTS = ((("z", 0, 1), ("z", 1, 1)), (("z", 2, 1),), (("z", 3, 1),), (("d", 1, 1),), (("e", 0, 0),), (("e", 0, 1),), (("d", 2, 0),), (("d", 2, 1),), (("d", 3, 0),), (("d", 3, 1),), (("e", 1, 0),), ())
+AFTER = ((), (("e", 1, 1),))
+SPLIT = True
 
 
 def tile_weighted_ista_step_f3_kernel(tc, z, d, x, prec, eta, lam, gain, out):
@@ -40,28 +40,39 @@ def tile_weighted_ista_step_f3_kernel(tc, z, d, x, prec, eta, lam, gain, out):
     with ExitStack() as ctx:
         keep = ctx.enter_context(tc.tile_pool(name="keep", bufs=1))
         raws = ctx.enter_context(tc.tile_pool(name="raws", bufs=11))
-        bigs = ctx.enter_context(tc.tile_pool(name="bigs", bufs=5))
-        grps = ctx.enter_context(tc.tile_pool(name="grps", bufs=6))
+        bigs = ctx.enter_context(tc.tile_pool(name="bigs", bufs=4))
+        grps = ctx.enter_context(tc.tile_pool(name="grps", bufs=5))
         zcs = ctx.enter_context(tc.tile_pool(name="zcs", bufs=4))
         es = ctx.enter_context(tc.tile_pool(name="es", bufs=2))
         vs = ctx.enter_context(tc.tile_pool(name="vs", bufs=8))
-        outs = ctx.enter_context(tc.tile_pool(name="outs", bufs=4))
+        outs = ctx.enter_context(tc.tile_pool(name="outs", bufs=6))
         acc = ctx.enter_context(tc.psum_pool(name="acc", bufs=4))
         turn = ctx.enter_context(tc.psum_pool(name="turn", bufs=4))
 
         ident = keep.tile([P, P], F32, name="ident")
         make_identity(nc, ident[:])
-        warm = keep.tile([P, 2], F32, name="warm")
-        nc.vector.memset(warm[:], 0.0)
-        nc.scalar.activation(warm[:, 1:2], warm[:, 0:1], ACT.Copy, scale=1.0)
-
-        ctx.enter_context(tc.manual_schedule())
-
-        consts = {}
+        scratch = keep.tile([P, 2], F32, name="scratch")
+        nc.vector.memset(scratch[:], 0.0)
+        nc.scalar.activation(scratch[:, 1:2], scratch[:, 0:1], ACT.Copy, scale=1.0)
         rows = keep.tile([P, W], BF16, name="rows", align_bytes=64)
+        nc.vector.memset(rows[:], 0.0)
+        prow = keep.tile([P, F], BF16, name="prow")
+        nc.vector.memset(prow[:], 0.0)
+        first_row = keep.tile([P, P], BF16, name="first_row")
+        nc.vector.memset(first_row[:], 0.0)
+        nc.vector.memset(first_row[0:1, :], 1.0)
         blank = keep.tile([P, W], BF16, name="blank")
         nc.vector.memset(blank[:], 0.0)
-        nc.vector.memset(rows[:], 0.0)
+        prec_all = keep.tile([P, F], F32, name="prec_all")
+
+        ctx.enter_context(tc.manual_schedule())
+        consts = {}
+        zraw, xraw, draw = {}, {}, {}
+        zT, zc, zs = {}, {}, {}
+        dg, dc, ds = {}, {}, {}
+        tg, tcod, tsc = {}, {}, {}
+        ew, eg, ec, esc = {}, {}, {}, {}
+        laid = {}
 
         def warm_up(n):
             bank = turn.tile([P, W], F32, name="bank")
@@ -69,25 +80,25 @@ def tile_weighted_ista_step_f3_kernel(tc, z, d, x, prec, eta, lam, gain, out):
                 nc.tensor.matmul(bank[:], lhsT=blank[:, 0:P], rhs=blank[:], start=True, stop=True)
 
         def load_rows():
-            for r, src in ((0, prec), (32, eta), (64, lam), (96, gain)):
+            nc.sync.dma_start(out=prow[0:1, :], in_=prec.unsqueeze(0))
+            for r, src in ((0, eta), (32, lam), (64, gain)):
                 v = src.rearrange("(g k) -> g k", k=W)
-                nc.sync.dma_start(out=rows[r:r + v.shape[0], :], in_=v)
+                nc.sync.dma_start(out=rows[r:r + CH, :], in_=v)
 
         def make_consts():
             words = rows[:].bitcast(F32)
             bank = turn.tile([P, 4, P], F32, name="bank")
             for u in range(2):
                 nc.tensor.transpose(bank[:, u, :], words[:, u:256:2], ident[:])
-            table = keep.tile([P, 100, 4], F32, name="table")
+            table = keep.tile([P, 68, 4], F32, name="table")
             for u in range(2):
                 pairs = bank[:, u, :].bitcast(BF16).rearrange("p (r e) -> p r e", e=2)
-                nc.vector.tensor_copy(out=table[:, :, 2 * u:2 * u + 2], in_=pairs[:, 0:100, :])
+                nc.vector.tensor_copy(out=table[:, :, 2 * u:2 * u + 2], in_=pairs[:, 0:68, :])
             c = consts
-            c["prec"] = table[:, 0:2, :]
-            c["eta"] = table[:, 32:36, :]
-            c["lam"] = table[:, 64:68, :]
-            c["gain"] = table[:, 96:100, :]
-            for name in ("neta", "th", "nth", "ngeta", "gth", "ngth", "ngain"):
+            c["eta"] = table[:, 0:4, :]
+            c["lam"] = table[:, 32:36, :]
+            c["gain"] = table[:, 64:68, :]
+            for name in ("neta", "th", "nth", "ngeta", "gth", "ngth", "gth2"):
                 t = keep.tile([P, CH, 4], F32, name=name + "_c")
                 c[name] = t[:]
             g = nc.gpsimd
@@ -96,18 +107,21 @@ def tile_weighted_ista_step_f3_kernel(tc, z, d, x, prec, eta, lam, gain, out):
             g.tensor_scalar(c["nth"], c["th"], -1.0, None, ALU.mult)
             g.tensor_tensor(c["ngeta"], c["neta"], c["gain"], ALU.mult)
 
+        def spread_prec():
+            for fg in range(FG):
+                bank = turn.tile([P, W], F32, name="bank")
+                nc.tensor.matmul(bank[:], lhsT=first_row[:], rhs=prow[:, fg * W:(fg + 1) * W], start=True, stop=True)
+                nc.vector.tensor_copy(
+                    out=prec_all[:, fg * W:(fg + 1) * W].rearrange("p (u w e) -> p u w e", u=2, e=2),
+                    in_=bank[:].rearrange("p (w u e) -> p u w e", u=2, e=2))
+
         def gain_thresholds():
             c = consts
             t = keep.tile([P, CH, 4], F32, name="absg")
             nc.vector.scalar_tensor_tensor(out=t[:], in0=c["gain"], scalar=-1.0, in1=c["gain"], op0=ALU.mult, op1=ALU.max)
             nc.vector.tensor_tensor(c["gth"], t[:], c["th"], ALU.mult)
             nc.vector.tensor_scalar(c["ngth"], c["gth"], -1.0, None, ALU.mult)
-
-        zraw, xraw, draw = {}, {}, {}
-        zT, zc, zs = {}, {}, {}
-        dg, dc, ds = {}, {}, {}
-        tg, tcod, tsc = {}, {}, {}
-        xp, eb, eg, ec, esc = {}, {}, {}, {}, {}
+            nc.vector.tensor_scalar(c["gth2"], c["gth"], 2.0, None, ALU.mult)
 
         def load_z(c, h):
             t = raws.tile([P, 4, W], BF16, name="raw")
@@ -124,46 +138,75 @@ def tile_weighted_ista_step_f3_kernel(tc, z, d, x, prec, eta, lam, gain, out):
             nc.sync.dma_start(out=t[:], in_=d[c * W:(c + 1) * W, :].rearrange("(p j) f -> p j f", j=4))
             draw[c] = t
 
-        laid = {}
-
-        def lay_words(kind, a, b):
+        def word_source(f):
+            kind, a, b = f
+            if kind == "z":
+                return zraw[a, b][:].bitcast(F32)
             if kind == "d":
-                src = draw[a][:].bitcast(F32)[:, :, 256 * b:256 * (b + 1)]
-            elif kind == "z":
-                src = zraw[a, b][:].bitcast(F32)
-            else:
-                src = xraw[a, b][:].bitcast(F32)
+                return draw[a][:].bitcast(F32)[:, :, 256 * b:256 * (b + 1)]
+            return ew[a, b][:].bitcast(F32)
+
+        def lay_words(f):
             t = raws.tile([P, 4, 2, P], F32, name="raw")
-            nc.vector.tensor_copy(out=t[:], in_=src.rearrange("p s (w u) -> p s u w", u=2))
-            laid[kind, a, b] = t
+            nc.scalar.copy(out=t[:], in_=word_source(f).rearrange("p s (w u) -> p s u w", u=2))
+            laid[f] = t
 
-        def words_of(kind, a, b, src, s, u):
-            if (kind, a, b) in laid:
-                return laid[kind, a, b][:, s, u, :]
-            return src[:, s, u:256:2]
-
-        def z_turn(c, h):
-            words = zraw[c, h][:].bitcast(F32)
-            t = keep.tile([P, W, 4], BF16, name="zT%d%d" % (c, h), align_bytes=64)
-            zT[c, h] = t
+        def turn_in(f):
+            kind, a, b = f
+            words = word_source(f)
+            if kind == "z":
+                t = keep.tile([P, W, 4], BF16, name="zT%d%d" % (a, b), align_bytes=64)
+                zT[a, b] = t
+            else:
+                t = grps.tile([P, W, 4], BF16, name="grp", align_bytes=64)
+                if kind == "d":
+                    tg[a, b] = t
+                else:
+                    eg[a, b] = t
             dst = t[:].bitcast(F32)
-            for b in range(2):
+            for half in range(2):
                 bank = turn.tile([P, 2, 2, P], F32, name="bank")
-                for s in range(2):
+                for k in range(2):
+                    s = 2 * half + k
                     for u in range(2):
-                        nc.tensor.transpose(bank[:, u, s, :], words_of("z", c, h, words, 2 * b + s, u), ident[:])
-                nc.scalar.copy(out=dst[:, 256 * b:256 * (b + 1), :], in_=bank[:].rearrange("p u s n -> p (s n) u"))
+                        if f in laid:
+                            src = laid[f][:, s, u, :]
+                        elif kind == "e":
+                            src = words[:, s, u * P:(u + 1) * P]
+                        else:
+                            src = words[:, s, u:256:2]
+                        nc.tensor.transpose(bank[:, u, k, :], src, ident[:])
+                nc.scalar.copy(out=dst[:, 256 * half:256 * (half + 1), :], in_=bank[:].rearrange("p u k n -> p (k n) u"))
 
-        def z_quant(c, h):
-            a = zcs.tile([P, W], U32, name="zcode", align_bytes=64)
-            b = zcs.tile([P, W], U8, name="zscale", align_bytes=64)
-            nc.vector.quantize_mx(out=a[:].bitcast(E4M3), scales=b[:], in_=zT[c, h][:].rearrange("p n t -> p (n t)"))
-            zc[c, h], zs[c, h] = a, b
+        def quant_in(f):
+            kind, a, b = f
+            if kind == "z":
+                q = zcs.tile([P, W], U32, name="zcode", align_bytes=64)
+                s = zcs.tile([P, W], U8, name="zscale", align_bytes=64)
+                src = zT[a, b]
+                zc[a, b], zs[a, b] = q, s
+            elif kind == "d":
+                q = keep.tile([P, W], U32, name="tc%d%d" % (a, b), align_bytes=64)
+                s = keep.tile([P, W], U8, name="ts%d%d" % (a, b), align_bytes=64)
+                src = tg[a, b]
+                tcod[a, b], tsc[a, b] = q, s
+            else:
+                q = keep.tile([P, W], U32, name="ec%d%d" % (a, b), align_bytes=64)
+                s = keep.tile([P, W], U8, name="es%d%d" % (a, b), align_bytes=64)
+                src = eg[a, b]
+                ec[a, b], esc[a, b] = q, s
+            fmt = E5M2 if kind == "e" else E4M3
+            nc.vector.quantize_mx(out=q[:].bitcast(fmt), scales=s[:], in_=src[:].rearrange("p n t -> p (n t)"))
 
         def d_lay(c, fg):
             t = grps.tile([P, W, 4], BF16, name="grp", align_bytes=64)
-            dst = t[:].rearrange("p (t m) j -> p t m j", t=4)
-            src = draw[c][:, :, fg * W:(fg + 1) * W].rearrange("p j (m t) -> p t m j", t=4)
+            src = draw[c][:, :, fg * W:(fg + 1) * W]
+            if FAST:
+                dst = t[:].rearrange("p (c i) j -> p c j i", i=4)
+                src = src.rearrange("p j (c i) -> p c j i", i=4)
+            else:
+                dst = t[:]
+                src = src.rearrange("p j f -> p f j")
             if (c, fg) in SCALAR_IL:
                 nc.scalar.copy(out=dst, in_=src)
             else:
@@ -176,75 +219,33 @@ def tile_weighted_ista_step_f3_kernel(tc, z, d, x, prec, eta, lam, gain, out):
             nc.vector.quantize_mx(out=a[:].bitcast(E4M3), scales=b[:], in_=dg[c, fg][:].rearrange("p n t -> p (n t)"))
             dc[c, fg], ds[c, fg] = a, b
 
-        def dt_turn(c, fg):
-            words = draw[c][:].bitcast(F32)[:, :, 256 * fg:256 * (fg + 1)]
-            t = grps.tile([P, W, 4], BF16, name="grp", align_bytes=64)
-            tg[c, fg] = t
-            dst = t[:].bitcast(F32)
-            for b in range(2):
-                bank = turn.tile([P, 2, 2, P], F32, name="bank")
-                for s in range(2):
-                    for u in range(2):
-                        nc.tensor.transpose(bank[:, u, s, :], words_of("d", c, fg, words, 2 * b + s, u), ident[:])
-                nc.scalar.copy(out=dst[:, 256 * b:256 * (b + 1), :], in_=bank[:].rearrange("p u s n -> p (s n) u"))
-
-        def dt_quant(c, fg):
-            a = keep.tile([P, W], U32, name="tc%d%d" % (c, fg), align_bytes=64)
-            b = keep.tile([P, W], U8, name="ts%d%d" % (c, fg), align_bytes=64)
-            nc.vector.quantize_mx(out=a[:].bitcast(E4M3), scales=b[:], in_=tg[c, fg][:].rearrange("p n t -> p (n t)"))
-            tcod[c, fg], tsc[c, fg] = a, b
-
-        def x_turn(h, fg):
-            words = xraw[h, fg][:].bitcast(F32)
-            t = bigs.tile([P, 4, W], F32, name="big")
-            xp[h, fg] = t
-            for u in range(2):
-                bank = turn.tile([P, 4, P], F32, name="bank")
-                for s in range(4):
-                    nc.tensor.transpose(bank[:, s, :], words_of("x", h, fg, words, s, u), ident[:])
-                pairs = bank[:].rearrange("p s n -> p (s n)").bitcast(BF16).rearrange("p (n e) -> p n e", e=2)
-                for e in range(2):
-                    k = 2 * u + e
-                    nc.scalar.activation(t[:, k, :], pairs[:, :, e], ACT.Copy, scale=consts["prec"][:, fg, k:k + 1])
-
-        def s1_pass(y, h, fg, t, c):
+        def s1_pass(y, h, fg, s, c):
             nc.tensor.matmul_mx(
                 out=y[:],
-                lhsT=dc[c, fg][:, t * P:(t + 1) * P].bitcast(E4M3),
-                lhsT_scale=ds[c, fg][:, t * P:(t + 1) * P],
-                rhs=zc[c, h][:].bitcast(E4M3),
-                rhs_scale=zs[c, h][:],
+                lhsT=zc[c, h][:, s * P:(s + 1) * P].bitcast(E4M3),
+                lhsT_scale=zs[c, h][:, s * P:(s + 1) * P],
+                rhs=dc[c, fg][:].bitcast(E4M3),
+                rhs_scale=ds[c, fg][:],
                 start=(c == 0),
                 stop=(c == CH - 1),
             )
 
-        def residual(y, h, fg, t):
-            if t == 0:
-                eb[h, fg] = es.tile([P, 4, W], BF16, name="ebf")
-            nc.vector.scalar_tensor_tensor(
-                out=eb[h, fg][:, t, :], in0=y[:], scalar=consts["prec"][:, fg, t:t + 1], in1=xp[h, fg][:, t, :],
-                op0=ALU.mult, op1=ALU.subtract)
+        def residual(y, h, fg, s):
+            if s == 0:
+                ew[h, fg] = es.tile([P, 4, W], BF16, name="ew")
+            r = vs.tile([P, W], F32, name="v")
+            nc.vector.tensor_tensor(
+                r[:].rearrange("p (u w e) -> p u w e", u=2, e=2),
+                y[:].rearrange("p (w u e) -> p u w e", u=2, e=2),
+                xraw[h, fg][:, s, :].rearrange("p (w u e) -> p u w e", u=2, e=2),
+                ALU.subtract)
+            nc.gpsimd.tensor_tensor(ew[h, fg][:, s, :], r[:], prec_all[:, fg * W:(fg + 1) * W], ALU.mult)
 
-        def e_lay(h, fg, engine):
-            t = grps.tile([P, W, 4], BF16, name="grp", align_bytes=64)
-            src = eb[h, fg][:].rearrange("p t n -> p n t")
-            if engine == "scalar":
-                nc.scalar.copy(out=t[:], in_=src)
-            else:
-                nc.vector.tensor_copy(out=t[:], in_=src)
-            eg[h, fg] = t
-
-        def e_quant(h, fg):
-            a = keep.tile([P, W], U32, name="ec%d%d" % (h, fg), align_bytes=64)
-            b = keep.tile([P, W], U8, name="ec_s%d%d" % (h, fg), align_bytes=64)
-            nc.vector.quantize_mx(out=a[:].bitcast(E5M2), scales=b[:], in_=eg[h, fg][:].rearrange("p n t -> p (n t)"))
-            ec[h, fg], esc[h, fg] = a, b
-
-        def s1_unit(h, fg, t):
+        def s1_unit(h, fg, s):
             y = acc.tile([P, W], F32, name="sums")
             for c in range(CH):
-                s1_pass(y, h, fg, t, c)
-            residual(y, h, fg, t)
+                s1_pass(y, h, fg, s, c)
+            residual(y, h, fg, s)
 
         leaf = {}
         pend = {}
@@ -279,40 +280,38 @@ def tile_weighted_ista_step_f3_kernel(tc, z, d, x, prec, eta, lam, gain, out):
             nc.vector.tensor_scalar(t[:, 1, :], v[:], col("nth", g, j), col("gain", g, j), ALU.min, ALU.mult)
             leaf[g, h, j] = (t[:, 0, :], t[:, 1, :])
 
-        made = {}
-
         def gain_z(g, h, j):
-            if KINDS[CH * h + g][j] == "K":
-                t = raws.tile([P, 2, W], F32, name="raw")
-                made[g, h, j] = t
-                dst = t[:, 0, :]
-            else:
-                v = vs.tile([P, W], F32, name="v")
-                dst = v[:]
-            pend[g, h, j] = dst
-            nc.gpsimd.tensor_scalar(dst, zT[g, h][:, :, j], col("gain", g, j), 0.0, ALU.mult, ALU.add)
+            v = vs.tile([P, W], F32, name="v")
+            pend[g, h, j] = v
+            nc.gpsimd.tensor_scalar(v[:], zT[g, h][:, :, j], col("gain", g, j), 0.0, ALU.mult, ALU.add)
+
+        def gain_z_down(g, h, j):
+            t = raws.tile([P, 2, W], F32, name="raw")
+            pend[g, h, j] = t
+            nc.gpsimd.tensor_scalar(t[:, 0, :], zT[g, h][:, :, j], col("gain", g, j), col("ngth", g, j), ALU.mult, ALU.add)
+
+        def step_down(y, g, h, j):
+            t = pend[g, h, j]
+            u, b = t[:, 0, :], t[:, 1, :]
+            nc.vector.scalar_tensor_tensor(
+                out=u, in0=y[:], scalar=col("ngeta", g, j), in1=u, op0=ALU.mult, op1=ALU.add)
+            a = vs.tile([P, W], F32, name="v")
+            nc.scalar.activation(a[:], u, ACT.Relu, bias=col("gth2", g, j))
+            nc.scalar.activation(b, a[:], ACT.Relu, bias=col("gth2", g, j), scale=-1.0)
+            leaf[g, h, j] = (u, b)
 
         def step_gained(y, g, h, j):
             v = pend[g, h, j]
             nc.vector.scalar_tensor_tensor(
-                out=v, in0=y[:], scalar=col("ngeta", g, j), in1=v, op0=ALU.mult, op1=ALU.add)
-            if KINDS[CH * h + g][j] == "K":
-                c = made[g, h, j][:, 1, :]
-                nc.scalar.activation(c, v, ACT.Copy, scale=-1.0)
-                leaf[g, h, j] = (v, c)
-            else:
-                r = vs.tile([P, W], F32, name="v")
-                nc.scalar.activation(r[:], v, ACT.Relu, bias=col("ngth", g, j))
-                pend[g, h, j] = (v, r)
-
-        def clamp(g, h, j):
-            c = leaf[g, h, j][1]
-            nc.gpsimd.tensor_scalar(c, c, col("gth", g, j), col("ngth", g, j), ALU.min, ALU.max)
+                out=v[:], in0=y[:], scalar=col("ngeta", g, j), in1=v[:], op0=ALU.mult, op1=ALU.add)
+            r = vs.tile([P, W], F32, name="v")
+            nc.scalar.activation(r[:], v[:], ACT.Relu, bias=col("ngth", g, j))
+            pend[g, h, j] = (v, r)
 
         def join_gained(g, h, j, dst):
             v, r = pend[g, h, j]
             nc.vector.scalar_tensor_tensor(
-                out=dst, in0=v, scalar=col("gth", g, j), in1=r[:], op0=ALU.add, op1=ALU.min)
+                out=dst, in0=v[:], scalar=col("gth", g, j), in1=r[:], op0=ALU.add, op1=ALU.min)
             leaf[g, h, j] = (dst,)
 
         def turn_out(g, h, s, engine):
@@ -333,25 +332,23 @@ def tile_weighted_ista_step_f3_kernel(tc, z, d, x, prec, eta, lam, gain, out):
             r = h * W + s * P
             nc.sync.dma_start(out=out[r:r + P, g * W:(g + 1) * W], in_=o[:])
 
-        def nothing():
-            return None
+        order = [(g, h) for h in range(HALVES) for g in range(CH)]
 
         def gain_ahead(n):
             if n < 8:
                 g, h = order[n]
                 for j in range(4):
-                    if KINDS[n][j] in "ZK":
+                    if KINDS[n][j] == "Z":
                         gain_z(g, h, j)
+                    elif KINDS[n][j] == "R":
+                        gain_z_down(g, h, j)
 
         def finish_unit(n, j, pair):
             g, h = order[n]
-            k = KINDS[n][j]
-            if k == "D":
+            if KINDS[n][j] == "D":
                 split_plain(g, h, j)
-            elif k == "K":
-                clamp(g, h, j)
-            else:
-                join_gained(g, h, j, pair[:, j // 2, :])
+            elif KINDS[n][j] == "Z":
+                join_gained(g, h, j, pair[:, j % 2, :])
 
         def group(n, between, after):
             g, h = order[n]
@@ -359,137 +356,106 @@ def tile_weighted_ista_step_f3_kernel(tc, z, d, x, prec, eta, lam, gain, out):
             pair = None
             if "Z" in kinds:
                 pair = raws.tile([P, 2, W], F32, name="raw")
-            gain_ahead(n + 1)
             for j in range(4):
                 y = s2_sums(g, h, j)
                 if kinds[j] == "D":
                     step_plain(y, g, h, j)
+                elif kinds[j] == "R":
+                    step_down(y, g, h, j)
                 else:
                     step_gained(y, g, h, j)
                 if j == 1:
                     between()
                 if j >= LAG:
                     finish_unit(n, j - LAG, pair)
+                if j == 2:
+                    gain_ahead(n + 1)
             for j in range(4 - LAG, 4):
                 finish_unit(n, j, pair)
             after()
 
-        load_z(0, 0)
-        load_rows()
-        load_d(0)
-        load_z(1, 0)
-        load_d(1)
-        load_z(2, 0)
-        load_d(2)
-        load_z(3, 0)
-        load_d(3)
-        load_x(0, 0)
-        load_x(0, 1)
-        for c in range(CH):
-            load_z(c, 1)
-        load_x(1, 0)
-        load_x(1, 1)
+        for name in LOADS.split(" "):
+            if name == "r":
+                load_rows()
+            elif name[0] == "z":
+                load_z(int(name[1]), int(name[2]))
+            elif name[0] == "x":
+                load_x(int(name[1]), int(name[2]))
+            else:
+                load_d(int(name[1]))
 
-        def sums():
-            y = acc.tile([P, W], F32, name="sums")
-            return y
-
-        order = [(g, h) for h in range(HALVES) for g in range(CH)]
-        turns = {"z": z_turn, "d": dt_turn, "x": x_turn}
-
-        def turn_in(f):
-            turns[f[0]](f[1], f[2])
-
-        def lay(f):
-            if LAYW:
-                lay_words(*f)
+        def lay_ahead(fs):
+            for f in fs:
+                if f in SCALAR_WORDS:
+                    lay_words(f)
 
         first = []
-        for t in range(4):
-            first.append(sums())
+        for s in range(4):
+            y = acc.tile([P, W], F32, name="sums")
+            first.append(y)
         warm_up(WARM0)
         make_consts()
         for c in range(CH):
-            z_turn(c, 0)
+            turn_in(("z", c, 0))
             warm_up(WARM[c])
             d_lay(c, 0)
-            z_quant(c, 0)
+            quant_in(("z", c, 0))
             d_quant(c, 0)
             d_lay(c, 1)
+            if c == 2:
+                spread_prec()
             if c > 0:
-                for t in range(4):
-                    s1_pass(first[t], 0, 0, t, c - 1)
+                for s in range(4):
+                    s1_pass(first[s], 0, 0, s, c - 1)
                 for f in HEAD[c - 1]:
-                    dt_turn(*f)
+                    turn_in(f)
             d_quant(c, 1)
             if c > 1:
                 for f in HEAD[c - 2]:
-                    dt_quant(*f)
-        x_turn(0, 0)
-        lay(SLOTS[0])
-        for t in range(4):
-            s1_pass(first[t], 0, 0, t, 3)
-            residual(first[t], 0, 0, t)
-        x_turn(0, 1)
+                    quant_in(f)
+        lay_ahead(SLOTS[0])
+        for s in range(4):
+            s1_pass(first[s], 0, 0, s, 3)
+            residual(first[s], 0, 0, s)
         for f in HEAD[2]:
-            dt_quant(*f)
+            quant_in(f)
         for n in range(12):
-            h, fg, t = ((0, 1), (1, 0), (1, 1))[n // 4] + (n % 4,)
-            if n + 1 < len(SLOTS):
-                lay(SLOTS[n + 1])
-            s1_unit(h, fg, t)
-            if n < len(SLOTS):
-                turn_in(SLOTS[n])
-            if n == 3:
-                turn_in(EXTRA)
-            if 0 < n <= len(SLOTS):
-                f = SLOTS[n - 1]
-                if f[0] == "z" and f[1] < 3:
-                    z_quant(f[1], f[2])
-                elif f[0] == "d":
-                    dt_quant(f[1], f[2])
-            if n == 3:
-                z_quant(3, 1)
-            if n == 0:
-                e_lay(0, 0, LAY[0])
+            h, fg, s = ((0, 1), (1, 0), (1, 1))[n // 4] + (n % 4,)
+            if n + 1 < 12:
+                lay_ahead(SLOTS[n + 1])
+            s1_unit(h, fg, s)
+            for f in SLOTS[n]:
+                turn_in(f)
+            if n > 0:
+                for f in SLOTS[n - 1]:
+                    if f[0] != "z" or n != 3:
+                        quant_in(f)
             if n == 2:
-                e_quant(0, 0)
-            if n == 4:
-                e_lay(0, 1, LAY[1])
-            if n == 6:
-                e_quant(0, 1)
+                for f in SLOTS[2]:
+                    quant_in(f)
             if n == 8:
-                e_lay(1, 0, LAY[2])
                 gain_thresholds()
             if n == 10:
-                e_quant(1, 0)
                 gain_ahead(0)
+        for f in SLOTS[11]:
+            quant_in(f)
 
-        for f in LATE[0]:
-            lay(f)
         for n in range(8):
             def between(n=n):
                 if SPLIT and n > 1:
                     for s in (2, 3):
-                        turn_out(*order[n - 2], s, "scalar")
-                if n < len(LATE):
-                    for f in LATE[n]:
+                        turn_out(*order[n - 2], s, OUT[s])
+                if n < len(AFTER):
+                    for f in AFTER[n]:
                         turn_in(f)
-                if 0 < n <= len(LATE):
-                    for f in LATE[n - 1]:
-                        dt_quant(f[1], f[2])
-                if n == 1:
-                    e_lay(1, 1, LAY[3])
-                if n == 2:
-                    e_quant(1, 1)
+                if 0 < n <= len(AFTER):
+                    for f in AFTER[n - 1]:
+                        quant_in(f)
 
             def after(n=n):
                 if n > 0:
                     for s in (0, 1) if SPLIT else range(4):
                         turn_out(*order[n - 1], s, OUT[s])
-            if 0 < n < len(LATE):
-                for f in LATE[n]:
-                    lay(f)
             group(n, between, after)
         if SPLIT:
             for s in (2, 3):

@@ -21,30 +21,33 @@ CH = P_ATOMS // W
 FG = F // W
 HALVES = M // W
 SCALAR_IL = ((1, 1), (2, 1), (3, 1))
-WARM0 = 6
-WARM = (2, 2, 1, 1)
-KINDS = ("DDDD",) * 8
-SCALAR_WORDS = (("z", 0, 1), ("z", 1, 1), ("z", 2, 1), ("z", 3, 1), ("d", 1, 1), ("d", 2, 0), ("d", 2, 1), ("d", 3, 0), ("d", 3, 1))
-FAST = True
+WARM0 = 10
+WARM = (0, 0, 3, 2)
+KINDS = ('EDDD', 'EDDD', 'EDDD', 'EDDD', 'EDDD', 'EDDD', 'EDDD', 'EDDD')
+VECTOR_WORDS = ()
+WORDS = (('d', 2, 0), ('d', 2, 1), ('d', 3, 0), ('d', 3, 1), ('z', 0, 1), ('z', 1, 1), ('z', 2, 1), ('z', 3, 1))
+VECTOR_COPIES = (('z', 1, 1),)
+VECTOR_WEIGHS = ((0, 1, 2), (1, 0, 1), (1, 1, 1))
+SPREAD = 0
 LAG = 2
-OUT = ("scalar",) * 4
-LOADS = "z00 r d0 z10 d1 z20 d2 x00 z30 d3 x01 z01 z11 z21 z31 x10 x11"
-HEAD = ((("d", 0, 0),), (("d", 0, 1),), (("d", 1, 0),))
-SLOTS = ((("z", 0, 1), ("z", 1, 1)), (("z", 2, 1),), (("z", 3, 1),), (("d", 1, 1),), (("e", 0, 0),), (("e", 0, 1),), (("d", 2, 0),), (("d", 2, 1),), (("d", 3, 0),), (("d", 3, 1),), (("e", 1, 0),), ())
-AFTER = ((), (("e", 1, 1),))
-SPLIT = True
+LAST = ('scalar', 'vector', 'scalar', 'vector')
+OUT = ('scalar', 'scalar', 'scalar', 'scalar')
+LOADS = 'z00 r d0 d1 z10 d2 d3 z01 x0 z11 x1'
+HEAD = ((('d', 1, 0),), (), (('d', 0, 0),))
+SLOTS = ((('z', 1, 1), ('z', 0, 1)), (('d', 0, 1), ('z', 2, 1)), (('z', 3, 1), ('d', 1, 1)), (('d', 2, 1),), (('e', 0, 0), ('e', 0, 1)), (), (), (), (('d', 3, 0), ('d', 3, 1)), (), (), ())
+AFTER = ((('d', 2, 0),), (('e', 1, 1), ('e', 1, 0)))
+SPLIT = False
 
 
 def tile_weighted_ista_step_f3_kernel(tc, z, d, x, prec, eta, lam, gain, out):
     nc = tc.nc
     with ExitStack() as ctx:
         keep = ctx.enter_context(tc.tile_pool(name="keep", bufs=1))
-        raws = ctx.enter_context(tc.tile_pool(name="raws", bufs=11))
-        bigs = ctx.enter_context(tc.tile_pool(name="bigs", bufs=4))
-        grps = ctx.enter_context(tc.tile_pool(name="grps", bufs=5))
+        bigs = ctx.enter_context(tc.tile_pool(name="bigs", bufs=9))
+        grps = ctx.enter_context(tc.tile_pool(name="grps", bufs=7))
         zcs = ctx.enter_context(tc.tile_pool(name="zcs", bufs=4))
         es = ctx.enter_context(tc.tile_pool(name="es", bufs=2))
-        vs = ctx.enter_context(tc.tile_pool(name="vs", bufs=8))
+        vs = ctx.enter_context(tc.tile_pool(name="vs", bufs=5))
         outs = ctx.enter_context(tc.tile_pool(name="outs", bufs=6))
         acc = ctx.enter_context(tc.psum_pool(name="acc", bufs=4))
         turn = ctx.enter_context(tc.psum_pool(name="turn", bufs=4))
@@ -56,7 +59,7 @@ def tile_weighted_ista_step_f3_kernel(tc, z, d, x, prec, eta, lam, gain, out):
         nc.scalar.activation(scratch[:, 1:2], scratch[:, 0:1], ACT.Copy, scale=1.0)
         rows = keep.tile([P, W], BF16, name="rows", align_bytes=64)
         nc.vector.memset(rows[:], 0.0)
-        prow = keep.tile([P, F], BF16, name="prow")
+        prow = es.tile([P, F], BF16, name="ew")
         nc.vector.memset(prow[:], 0.0)
         first_row = keep.tile([P, P], BF16, name="first_row")
         nc.vector.memset(first_row[:], 0.0)
@@ -72,12 +75,12 @@ def tile_weighted_ista_step_f3_kernel(tc, z, d, x, prec, eta, lam, gain, out):
         dg, dc, ds = {}, {}, {}
         tg, tcod, tsc = {}, {}, {}
         ew, eg, ec, esc = {}, {}, {}, {}
-        laid = {}
 
         def warm_up(n):
-            bank = turn.tile([P, W], F32, name="bank")
-            for k in range(n):
-                nc.tensor.matmul(bank[:], lhsT=blank[:, 0:P], rhs=blank[:], start=True, stop=True)
+            if n:
+                bank = turn.tile([P, W], F32, name="bank")
+                for k in range(n):
+                    nc.tensor.matmul(bank[:], lhsT=blank[:, 0:P], rhs=blank[:], start=True, stop=True)
 
         def load_rows():
             nc.sync.dma_start(out=prow[0:1, :], in_=prec.unsqueeze(0))
@@ -98,14 +101,14 @@ def tile_weighted_ista_step_f3_kernel(tc, z, d, x, prec, eta, lam, gain, out):
             c["eta"] = table[:, 0:4, :]
             c["lam"] = table[:, 32:36, :]
             c["gain"] = table[:, 64:68, :]
-            for name in ("neta", "th", "nth", "ngeta", "gth", "ngth", "gth2"):
+            for name in ("neta", "th", "nth", "hth"):
                 t = keep.tile([P, CH, 4], F32, name=name + "_c")
                 c[name] = t[:]
             g = nc.gpsimd
             g.tensor_scalar(c["neta"], c["eta"], -1.0, None, ALU.mult)
             g.tensor_tensor(c["th"], c["eta"], c["lam"], ALU.mult)
             g.tensor_scalar(c["nth"], c["th"], -1.0, None, ALU.mult)
-            g.tensor_tensor(c["ngeta"], c["neta"], c["gain"], ALU.mult)
+            g.tensor_tensor(c["hth"], c["gain"], c["th"], ALU.mult)
 
         def spread_prec():
             for fg in range(FG):
@@ -115,75 +118,83 @@ def tile_weighted_ista_step_f3_kernel(tc, z, d, x, prec, eta, lam, gain, out):
                     out=prec_all[:, fg * W:(fg + 1) * W].rearrange("p (u w e) -> p u w e", u=2, e=2),
                     in_=bank[:].rearrange("p (w u e) -> p u w e", u=2, e=2))
 
-        def gain_thresholds():
-            c = consts
-            t = keep.tile([P, CH, 4], F32, name="absg")
-            nc.vector.scalar_tensor_tensor(out=t[:], in0=c["gain"], scalar=-1.0, in1=c["gain"], op0=ALU.mult, op1=ALU.max)
-            nc.vector.tensor_tensor(c["gth"], t[:], c["th"], ALU.mult)
-            nc.vector.tensor_scalar(c["ngth"], c["gth"], -1.0, None, ALU.mult)
-            nc.vector.tensor_scalar(c["gth2"], c["gth"], 2.0, None, ALU.mult)
+        def load_z(cp, h):
+            t = bigs.tile([P, 4, 2 * W], BF16, name="big")
+            src = z[h * W:(h + 1) * W, cp * 2 * W:(cp + 1) * 2 * W]
+            nc.sync.dma_start(out=t[:], in_=src.rearrange("(s p) k -> p s k", p=P))
+            zraw[cp, h] = t
 
-        def load_z(c, h):
-            t = raws.tile([P, 4, W], BF16, name="raw")
-            nc.sync.dma_start(out=t[:], in_=z[h * W:(h + 1) * W, c * W:(c + 1) * W].rearrange("(s p) k -> p s k", p=P))
-            zraw[c, h] = t
-
-        def load_x(h, fg):
-            t = raws.tile([P, 4, W], BF16, name="raw")
-            nc.sync.dma_start(out=t[:], in_=x[h * W:(h + 1) * W, fg * W:(fg + 1) * W].rearrange("(s p) k -> p s k", p=P))
-            xraw[h, fg] = t
+        def load_x(h):
+            t = bigs.tile([P, 4, F], BF16, name="big")
+            nc.sync.dma_start(out=t[:], in_=x[h * W:(h + 1) * W, :].rearrange("(s p) k -> p s k", p=P))
+            xraw[h] = t
 
         def load_d(c):
             t = bigs.tile([P, 4, F], BF16, name="big")
             nc.sync.dma_start(out=t[:], in_=d[c * W:(c + 1) * W, :].rearrange("(p j) f -> p j f", j=4))
             draw[c] = t
 
-        def word_source(f):
-            kind, a, b = f
-            if kind == "z":
-                return zraw[a, b][:].bitcast(F32)
-            if kind == "d":
-                return draw[a][:].bitcast(F32)[:, :, 256 * b:256 * (b + 1)]
-            return ew[a, b][:].bitcast(F32)
+        laid = {}
 
         def lay_words(f):
-            t = raws.tile([P, 4, 2, P], F32, name="raw")
-            nc.scalar.copy(out=t[:], in_=word_source(f).rearrange("p s (w u) -> p s u w", u=2))
+            kind, a, b = f
+            t = grps.tile([P, 4, 2, P], F32, name="grp", align_bytes=64)
+            if kind == "d":
+                src = draw[a][:].bitcast(F32)[:, :, 256 * b:256 * (b + 1)]
+            else:
+                src = zraw[a // 2, b][:].bitcast(F32)[:, :, 256 * (a % 2):256 * (a % 2 + 1)]
+            src = src.rearrange("p s (w u) -> p s u w", u=2)
+            if f in VECTOR_WORDS:
+                nc.vector.tensor_copy(out=t[:], in_=src)
+            else:
+                nc.scalar.copy(out=t[:], in_=src)
             laid[f] = t
 
-        def turn_in(f):
+        def turned(f):
             kind, a, b = f
-            words = word_source(f)
             if kind == "z":
-                t = keep.tile([P, W, 4], BF16, name="zT%d%d" % (a, b), align_bytes=64)
-                zT[a, b] = t
-            else:
+                if f not in zT:
+                    t = keep.tile([P, W, 4], BF16, name="zT%d%d" % (a, b), align_bytes=64)
+                    zT[f] = t
+                return zT[f]
+            home = tg if kind == "d" else eg
+            if (a, b) not in home:
                 t = grps.tile([P, W, 4], BF16, name="grp", align_bytes=64)
-                if kind == "d":
-                    tg[a, b] = t
-                else:
-                    eg[a, b] = t
-            dst = t[:].bitcast(F32)
-            for half in range(2):
-                bank = turn.tile([P, 2, 2, P], F32, name="bank")
-                for k in range(2):
-                    s = 2 * half + k
-                    for u in range(2):
-                        if f in laid:
-                            src = laid[f][:, s, u, :]
-                        elif kind == "e":
-                            src = words[:, s, u * P:(u + 1) * P]
-                        else:
-                            src = words[:, s, u:256:2]
-                        nc.tensor.transpose(bank[:, u, k, :], src, ident[:])
-                nc.scalar.copy(out=dst[:, 256 * half:256 * (half + 1), :], in_=bank[:].rearrange("p u k n -> p (k n) u"))
+                home[a, b] = t
+            return home[a, b]
+
+        def turn_half(f, half):
+            kind, a, b = f
+            t = turned(f)
+            bank = turn.tile([P, 2, 2, P], F32, name="bank")
+            for k in range(2):
+                for u in range(2):
+                    if f in laid:
+                        src = laid[f][:, 2 * half + k, u, :]
+                    elif kind == "z":
+                        src = zraw[a // 2, b][:].bitcast(F32)[:, 2 * half + k, 256 * (a % 2) + u:256 * (a % 2 + 1):2]
+                    elif kind == "d":
+                        src = draw[a][:].bitcast(F32)[:, 2 * half + k, 256 * b + u:256 * (b + 1):2]
+                    else:
+                        src = ew[a, b][:].bitcast(F32)[:, 2 * half + k, u * P:(u + 1) * P]
+                    nc.tensor.transpose(bank[:, u, k, :], src, ident[:])
+            dst = t[:].bitcast(F32)[:, 256 * half:256 * (half + 1), :]
+            src = bank[:].rearrange("p u k n -> p (k n) u")
+            if half == 1 and f in VECTOR_COPIES:
+                nc.vector.tensor_copy(out=dst, in_=src)
+            else:
+                nc.scalar.copy(out=dst, in_=src)
+
+        def turn_in(f):
+            turn_half(f, 0)
+            turn_half(f, 1)
 
         def quant_in(f):
             kind, a, b = f
             if kind == "z":
                 q = zcs.tile([P, W], U32, name="zcode", align_bytes=64)
                 s = zcs.tile([P, W], U8, name="zscale", align_bytes=64)
-                src = zT[a, b]
+                src = zT[f]
                 zc[a, b], zs[a, b] = q, s
             elif kind == "d":
                 q = keep.tile([P, W], U32, name="tc%d%d" % (a, b), align_bytes=64)
@@ -198,15 +209,17 @@ def tile_weighted_ista_step_f3_kernel(tc, z, d, x, prec, eta, lam, gain, out):
             fmt = E5M2 if kind == "e" else E4M3
             nc.vector.quantize_mx(out=q[:].bitcast(fmt), scales=s[:], in_=src[:].rearrange("p n t -> p (n t)"))
 
+        done = []
+
+        def quant_once(f):
+            if f not in done:
+                done.append(f)
+                quant_in(f)
+
         def d_lay(c, fg):
             t = grps.tile([P, W, 4], BF16, name="grp", align_bytes=64)
-            src = draw[c][:, :, fg * W:(fg + 1) * W]
-            if FAST:
-                dst = t[:].rearrange("p (c i) j -> p c j i", i=4)
-                src = src.rearrange("p j (c i) -> p c j i", i=4)
-            else:
-                dst = t[:]
-                src = src.rearrange("p j f -> p f j")
+            dst = t[:].rearrange("p (c i) j -> p c j i", i=4)
+            src = draw[c][:, :, fg * W:(fg + 1) * W].rearrange("p j (c i) -> p c j i", i=4)
             if (c, fg) in SCALAR_IL:
                 nc.scalar.copy(out=dst, in_=src)
             else:
@@ -237,9 +250,10 @@ def tile_weighted_ista_step_f3_kernel(tc, z, d, x, prec, eta, lam, gain, out):
             nc.vector.tensor_tensor(
                 r[:].rearrange("p (u w e) -> p u w e", u=2, e=2),
                 y[:].rearrange("p (w u e) -> p u w e", u=2, e=2),
-                xraw[h, fg][:, s, :].rearrange("p (w u e) -> p u w e", u=2, e=2),
+                xraw[h][:, s, fg * W:(fg + 1) * W].rearrange("p (w u e) -> p u w e", u=2, e=2),
                 ALU.subtract)
-            nc.gpsimd.tensor_tensor(ew[h, fg][:, s, :], r[:], prec_all[:, fg * W:(fg + 1) * W], ALU.mult)
+            weigh = nc.vector.tensor_tensor if (h, fg, s) in VECTOR_WEIGHS else nc.gpsimd.tensor_tensor
+            weigh(ew[h, fg][:, s, :], r[:], prec_all[:, fg * W:(fg + 1) * W], ALU.mult)
 
         def s1_unit(h, fg, s):
             y = acc.tile([P, W], F32, name="sums")
@@ -267,61 +281,33 @@ def tile_weighted_ista_step_f3_kernel(tc, z, d, x, prec, eta, lam, gain, out):
         def col(name, g, j):
             return consts[name][:, g, j:j + 1]
 
-        def step_plain(y, g, h, j):
+        def gradient_step(y, g, h, j):
             v = vs.tile([P, W], F32, name="v")
             nc.vector.scalar_tensor_tensor(
-                out=v[:], in0=y[:], scalar=col("neta", g, j), in1=zT[g, h][:, :, j], op0=ALU.mult, op1=ALU.add)
+                out=v[:], in0=y[:], scalar=col("neta", g, j), in1=zT["z", g, h][:, :, j], op0=ALU.mult, op1=ALU.add)
             pend[g, h, j] = v
 
-        def split_plain(g, h, j):
+        def split(g, h, j, kind):
             v = pend[g, h, j]
-            t = raws.tile([P, 2, W], F32, name="raw")
-            nc.vector.tensor_scalar(t[:, 0, :], v[:], col("th", g, j), col("gain", g, j), ALU.max, ALU.mult)
+            if j % 2 == 0:
+                t = bigs.tile([P, 2, 2, W], F32, name="big")
+                leaf[g, h, j] = t[:, 0]
+                leaf[g, h, j + 1] = t[:, 1]
+            t = leaf[g, h, j]
+            if kind == "E":
+                nc.scalar.activation(t[:, 0, :], v[:], ACT.Relu, bias=col("nth", g, j))
+                nc.scalar.activation(t[:, 0, :], t[:, 0, :], ACT.Identity, scale=col("gain", g, j), bias=col("hth", g, j))
+            else:
+                nc.vector.tensor_scalar(t[:, 0, :], v[:], col("th", g, j), col("gain", g, j), ALU.max, ALU.mult)
             nc.vector.tensor_scalar(t[:, 1, :], v[:], col("nth", g, j), col("gain", g, j), ALU.min, ALU.mult)
-            leaf[g, h, j] = (t[:, 0, :], t[:, 1, :])
-
-        def gain_z(g, h, j):
-            v = vs.tile([P, W], F32, name="v")
-            pend[g, h, j] = v
-            nc.gpsimd.tensor_scalar(v[:], zT[g, h][:, :, j], col("gain", g, j), 0.0, ALU.mult, ALU.add)
-
-        def gain_z_down(g, h, j):
-            t = raws.tile([P, 2, W], F32, name="raw")
-            pend[g, h, j] = t
-            nc.gpsimd.tensor_scalar(t[:, 0, :], zT[g, h][:, :, j], col("gain", g, j), col("ngth", g, j), ALU.mult, ALU.add)
-
-        def step_down(y, g, h, j):
-            t = pend[g, h, j]
-            u, b = t[:, 0, :], t[:, 1, :]
-            nc.vector.scalar_tensor_tensor(
-                out=u, in0=y[:], scalar=col("ngeta", g, j), in1=u, op0=ALU.mult, op1=ALU.add)
-            a = vs.tile([P, W], F32, name="v")
-            nc.scalar.activation(a[:], u, ACT.Relu, bias=col("gth2", g, j))
-            nc.scalar.activation(b, a[:], ACT.Relu, bias=col("gth2", g, j), scale=-1.0)
-            leaf[g, h, j] = (u, b)
-
-        def step_gained(y, g, h, j):
-            v = pend[g, h, j]
-            nc.vector.scalar_tensor_tensor(
-                out=v[:], in0=y[:], scalar=col("ngeta", g, j), in1=v[:], op0=ALU.mult, op1=ALU.add)
-            r = vs.tile([P, W], F32, name="v")
-            nc.scalar.activation(r[:], v[:], ACT.Relu, bias=col("ngth", g, j))
-            pend[g, h, j] = (v, r)
-
-        def join_gained(g, h, j, dst):
-            v, r = pend[g, h, j]
-            nc.vector.scalar_tensor_tensor(
-                out=dst, in0=v[:], scalar=col("gth", g, j), in1=r[:], op0=ALU.add, op1=ALU.min)
-            leaf[g, h, j] = (dst,)
 
         def turn_out(g, h, s, engine):
             bank = turn.tile([P, 4, P], F32, name="bank")
             cols = slice(s * P, (s + 1) * P)
             for j in range(4):
-                parts = leaf[g, h, j]
-                for k in range(len(parts)):
-                    nc.tensor.matmul(bank[:, j, :], lhsT=parts[k][:, cols], rhs=ident[:], is_transpose=True,
-                                     start=(k == 0), stop=(k == len(parts) - 1))
+                for k in range(2):
+                    nc.tensor.matmul(bank[:, j, :], lhsT=leaf[g, h, j][:, k, cols], rhs=ident[:], is_transpose=True,
+                                     start=(k == 0), stop=(k == 1))
             o = outs.tile([P, W], F32, name="o")
             src = bank[:].rearrange("p j n -> p n j")
             dst = o[:].rearrange("p (n j) -> p n j", j=4)
@@ -334,44 +320,16 @@ def tile_weighted_ista_step_f3_kernel(tc, z, d, x, prec, eta, lam, gain, out):
 
         order = [(g, h) for h in range(HALVES) for g in range(CH)]
 
-        def gain_ahead(n):
-            if n < 8:
-                g, h = order[n]
-                for j in range(4):
-                    if KINDS[n][j] == "Z":
-                        gain_z(g, h, j)
-                    elif KINDS[n][j] == "R":
-                        gain_z_down(g, h, j)
-
-        def finish_unit(n, j, pair):
-            g, h = order[n]
-            if KINDS[n][j] == "D":
-                split_plain(g, h, j)
-            elif KINDS[n][j] == "Z":
-                join_gained(g, h, j, pair[:, j % 2, :])
-
         def group(n, between, after):
             g, h = order[n]
-            kinds = KINDS[n]
-            pair = None
-            if "Z" in kinds:
-                pair = raws.tile([P, 2, W], F32, name="raw")
             for j in range(4):
-                y = s2_sums(g, h, j)
-                if kinds[j] == "D":
-                    step_plain(y, g, h, j)
-                elif kinds[j] == "R":
-                    step_down(y, g, h, j)
-                else:
-                    step_gained(y, g, h, j)
+                gradient_step(s2_sums(g, h, j), g, h, j)
                 if j == 1:
                     between()
                 if j >= LAG:
-                    finish_unit(n, j - LAG, pair)
-                if j == 2:
-                    gain_ahead(n + 1)
+                    split(g, h, j - LAG, KINDS[n][j - LAG])
             for j in range(4 - LAG, 4):
-                finish_unit(n, j, pair)
+                split(g, h, j, KINDS[n][j])
             after()
 
         for name in LOADS.split(" "):
@@ -380,14 +338,9 @@ def tile_weighted_ista_step_f3_kernel(tc, z, d, x, prec, eta, lam, gain, out):
             elif name[0] == "z":
                 load_z(int(name[1]), int(name[2]))
             elif name[0] == "x":
-                load_x(int(name[1]), int(name[2]))
+                load_x(int(name[1]))
             else:
                 load_d(int(name[1]))
-
-        def lay_ahead(fs):
-            for f in fs:
-                if f in SCALAR_WORDS:
-                    lay_words(f)
 
         first = []
         for s in range(4):
@@ -402,7 +355,7 @@ def tile_weighted_ista_step_f3_kernel(tc, z, d, x, prec, eta, lam, gain, out):
             quant_in(("z", c, 0))
             d_quant(c, 0)
             d_lay(c, 1)
-            if c == 2:
+            if c == SPREAD:
                 spread_prec()
             if c > 0:
                 for s in range(4):
@@ -413,6 +366,12 @@ def tile_weighted_ista_step_f3_kernel(tc, z, d, x, prec, eta, lam, gain, out):
             if c > 1:
                 for f in HEAD[c - 2]:
                     quant_in(f)
+
+        def lay_ahead(fs):
+            for f in fs:
+                if f in WORDS or f in VECTOR_WORDS:
+                    lay_words(f)
+
         lay_ahead(SLOTS[0])
         for s in range(4):
             s1_pass(first[s], 0, 0, s, 3)
@@ -428,15 +387,11 @@ def tile_weighted_ista_step_f3_kernel(tc, z, d, x, prec, eta, lam, gain, out):
                 turn_in(f)
             if n > 0:
                 for f in SLOTS[n - 1]:
-                    if f[0] != "z" or n != 3:
-                        quant_in(f)
-            if n == 2:
-                for f in SLOTS[2]:
-                    quant_in(f)
-            if n == 8:
-                gain_thresholds()
-            if n == 10:
-                gain_ahead(0)
+                    quant_once(f)
+            if n == 3:
+                for f in SLOTS[3]:
+                    if f[0] == "z":
+                        quant_once(f)
         for f in SLOTS[11]:
             quant_in(f)
 
@@ -461,4 +416,4 @@ def tile_weighted_ista_step_f3_kernel(tc, z, d, x, prec, eta, lam, gain, out):
             for s in (2, 3):
                 turn_out(*order[6], s, "scalar")
         for s in range(4):
-            turn_out(*order[7], s, "scalar" if s % 2 == 0 else "vector")
+            turn_out(*order[7], s, LAST[s])

from contextlib import ExitStack

import concourse.mybir as mybir
from concourse.masks import make_identity

M, P_ATOMS, F = 1024, 2048, 1024
FLOPS = 2 * 2 * M * P_ATOMS * F

F32 = mybir.dt.float32
BF16 = mybir.dt.bfloat16
U32 = mybir.dt.uint32
U8 = mybir.dt.uint8
E4M3 = mybir.dt.float8_e4m3fn_x4
E5M2 = mybir.dt.float8_e5m2_x4
ALU = mybir.AluOpType
ACT = mybir.ActivationFunctionType

P = 128
W = 512
CH = P_ATOMS // W
FG = F // W
HALVES = M // W
SCALAR_IL = ((1, 1), (2, 1), (3, 1))
WARM0 = 10
WARM = (0, 0, 3, 2)
KINDS = ('EDDD', 'EDDD', 'EDDD', 'EDDD', 'EDDD', 'EDDD', 'EDDD', 'EDDD')
VECTOR_WORDS = ()
WORDS = (('d', 2, 0), ('d', 2, 1), ('d', 3, 0), ('d', 3, 1), ('z', 0, 1), ('z', 1, 1), ('z', 2, 1), ('z', 3, 1))
VECTOR_COPIES = (('z', 1, 1),)
VECTOR_WEIGHS = ((0, 1, 2), (1, 0, 1), (1, 1, 1))
SPREAD = 0
LAG = 2
LAST = ('scalar', 'vector', 'scalar', 'vector')
OUT = ('scalar', 'scalar', 'scalar', 'scalar')
LOADS = 'z00 r d0 d1 z10 d2 d3 z01 x0 z11 x1'
HEAD = ((('d', 1, 0),), (), (('d', 0, 0),))
SLOTS = ((('z', 1, 1), ('z', 0, 1)), (('d', 0, 1), ('z', 2, 1)), (('z', 3, 1), ('d', 1, 1)), (('d', 2, 1),), (('e', 0, 0), ('e', 0, 1)), (), (), (), (('d', 3, 0), ('d', 3, 1)), (), (), ())
AFTER = ((('d', 2, 0),), (('e', 1, 1), ('e', 1, 0)))
SPLIT = False


def tile_weighted_ista_step_f3_kernel(tc, z, d, x, prec, eta, lam, gain, out):
    nc = tc.nc
    with ExitStack() as ctx:
        keep = ctx.enter_context(tc.tile_pool(name="keep", bufs=1))
        bigs = ctx.enter_context(tc.tile_pool(name="bigs", bufs=9))
        grps = ctx.enter_context(tc.tile_pool(name="grps", bufs=7))
        zcs = ctx.enter_context(tc.tile_pool(name="zcs", bufs=4))
        es = ctx.enter_context(tc.tile_pool(name="es", bufs=2))
        vs = ctx.enter_context(tc.tile_pool(name="vs", bufs=5))
        outs = ctx.enter_context(tc.tile_pool(name="outs", bufs=6))
        acc = ctx.enter_context(tc.psum_pool(name="acc", bufs=4))
        turn = ctx.enter_context(tc.psum_pool(name="turn", bufs=4))

        ident = keep.tile([P, P], F32, name="ident")
        make_identity(nc, ident[:])
        scratch = keep.tile([P, 2], F32, name="scratch")
        nc.vector.memset(scratch[:], 0.0)
        nc.scalar.activation(scratch[:, 1:2], scratch[:, 0:1], ACT.Copy, scale=1.0)
        rows = keep.tile([P, W], BF16, name="rows", align_bytes=64)
        nc.vector.memset(rows[:], 0.0)
        prow = es.tile([P, F], BF16, name="ew")
        nc.vector.memset(prow[:], 0.0)
        first_row = keep.tile([P, P], BF16, name="first_row")
        nc.vector.memset(first_row[:], 0.0)
        nc.vector.memset(first_row[0:1, :], 1.0)
        blank = keep.tile([P, W], BF16, name="blank")
        nc.vector.memset(blank[:], 0.0)
        prec_all = keep.tile([P, F], F32, name="prec_all")

        ctx.enter_context(tc.manual_schedule())
        consts = {}
        zraw, xraw, draw = {}, {}, {}
        zT, zc, zs = {}, {}, {}
        dg, dc, ds = {}, {}, {}
        tg, tcod, tsc = {}, {}, {}
        ew, eg, ec, esc = {}, {}, {}, {}

        def warm_up(n):
            if n:
                bank = turn.tile([P, W], F32, name="bank")
                for k in range(n):
                    nc.tensor.matmul(bank[:], lhsT=blank[:, 0:P], rhs=blank[:], start=True, stop=True)

        def load_rows():
            nc.sync.dma_start(out=prow[0:1, :], in_=prec.unsqueeze(0))
            for r, src in ((0, eta), (32, lam), (64, gain)):
                v = src.rearrange("(g k) -> g k", k=W)
                nc.sync.dma_start(out=rows[r:r + CH, :], in_=v)

        def make_consts():
            words = rows[:].bitcast(F32)
            bank = turn.tile([P, 4, P], F32, name="bank")
            for u in range(2):
                nc.tensor.transpose(bank[:, u, :], words[:, u:256:2], ident[:])
            table = keep.tile([P, 68, 4], F32, name="table")
            for u in range(2):
                pairs = bank[:, u, :].bitcast(BF16).rearrange("p (r e) -> p r e", e=2)
                nc.vector.tensor_copy(out=table[:, :, 2 * u:2 * u + 2], in_=pairs[:, 0:68, :])
            c = consts
            c["eta"] = table[:, 0:4, :]
            c["lam"] = table[:, 32:36, :]
            c["gain"] = table[:, 64:68, :]
            for name in ("neta", "th", "nth", "hth"):
                t = keep.tile([P, CH, 4], F32, name=name + "_c")
                c[name] = t[:]
            g = nc.gpsimd
            g.tensor_scalar(c["neta"], c["eta"], -1.0, None, ALU.mult)
            g.tensor_tensor(c["th"], c["eta"], c["lam"], ALU.mult)
            g.tensor_scalar(c["nth"], c["th"], -1.0, None, ALU.mult)
            g.tensor_tensor(c["hth"], c["gain"], c["th"], ALU.mult)

        def spread_prec():
            for fg in range(FG):
                bank = turn.tile([P, W], F32, name="bank")
                nc.tensor.matmul(bank[:], lhsT=first_row[:], rhs=prow[:, fg * W:(fg + 1) * W], start=True, stop=True)
                nc.vector.tensor_copy(
                    out=prec_all[:, fg * W:(fg + 1) * W].rearrange("p (u w e) -> p u w e", u=2, e=2),
                    in_=bank[:].rearrange("p (w u e) -> p u w e", u=2, e=2))

        def load_z(cp, h):
            t = bigs.tile([P, 4, 2 * W], BF16, name="big")
            src = z[h * W:(h + 1) * W, cp * 2 * W:(cp + 1) * 2 * W]
            nc.sync.dma_start(out=t[:], in_=src.rearrange("(s p) k -> p s k", p=P))
            zraw[cp, h] = t

        def load_x(h):
            t = bigs.tile([P, 4, F], BF16, name="big")
            nc.sync.dma_start(out=t[:], in_=x[h * W:(h + 1) * W, :].rearrange("(s p) k -> p s k", p=P))
            xraw[h] = t

        def load_d(c):
            t = bigs.tile([P, 4, F], BF16, name="big")
            nc.sync.dma_start(out=t[:], in_=d[c * W:(c + 1) * W, :].rearrange("(p j) f -> p j f", j=4))
            draw[c] = t

        laid = {}

        def lay_words(f):
            kind, a, b = f
            t = grps.tile([P, 4, 2, P], F32, name="grp", align_bytes=64)
            if kind == "d":
                src = draw[a][:].bitcast(F32)[:, :, 256 * b:256 * (b + 1)]
            else:
                src = zraw[a // 2, b][:].bitcast(F32)[:, :, 256 * (a % 2):256 * (a % 2 + 1)]
            src = src.rearrange("p s (w u) -> p s u w", u=2)
            if f in VECTOR_WORDS:
                nc.vector.tensor_copy(out=t[:], in_=src)
            else:
                nc.scalar.copy(out=t[:], in_=src)
            laid[f] = t

        def turned(f):
            kind, a, b = f
            if kind == "z":
                if f not in zT:
                    t = keep.tile([P, W, 4], BF16, name="zT%d%d" % (a, b), align_bytes=64)
                    zT[f] = t
                return zT[f]
            home = tg if kind == "d" else eg
            if (a, b) not in home:
                t = grps.tile([P, W, 4], BF16, name="grp", align_bytes=64)
                home[a, b] = t
            return home[a, b]

        def turn_half(f, half):
            kind, a, b = f
            t = turned(f)
            bank = turn.tile([P, 2, 2, P], F32, name="bank")
            for k in range(2):
                for u in range(2):
                    if f in laid:
                        src = laid[f][:, 2 * half + k, u, :]
                    elif kind == "z":
                        src = zraw[a // 2, b][:].bitcast(F32)[:, 2 * half + k, 256 * (a % 2) + u:256 * (a % 2 + 1):2]
                    elif kind == "d":
                        src = draw[a][:].bitcast(F32)[:, 2 * half + k, 256 * b + u:256 * (b + 1):2]
                    else:
                        src = ew[a, b][:].bitcast(F32)[:, 2 * half + k, u * P:(u + 1) * P]
                    nc.tensor.transpose(bank[:, u, k, :], src, ident[:])
            dst = t[:].bitcast(F32)[:, 256 * half:256 * (half + 1), :]
            src = bank[:].rearrange("p u k n -> p (k n) u")
            if half == 1 and f in VECTOR_COPIES:
                nc.vector.tensor_copy(out=dst, in_=src)
            else:
                nc.scalar.copy(out=dst, in_=src)

        def turn_in(f):
            turn_half(f, 0)
            turn_half(f, 1)

        def quant_in(f):
            kind, a, b = f
            if kind == "z":
                q = zcs.tile([P, W], U32, name="zcode", align_bytes=64)
                s = zcs.tile([P, W], U8, name="zscale", align_bytes=64)
                src = zT[f]
                zc[a, b], zs[a, b] = q, s
            elif kind == "d":
                q = keep.tile([P, W], U32, name="tc%d%d" % (a, b), align_bytes=64)
                s = keep.tile([P, W], U8, name="ts%d%d" % (a, b), align_bytes=64)
                src = tg[a, b]
                tcod[a, b], tsc[a, b] = q, s
            else:
                q = keep.tile([P, W], U32, name="ec%d%d" % (a, b), align_bytes=64)
                s = keep.tile([P, W], U8, name="es%d%d" % (a, b), align_bytes=64)
                src = eg[a, b]
                ec[a, b], esc[a, b] = q, s
            fmt = E5M2 if kind == "e" else E4M3
            nc.vector.quantize_mx(out=q[:].bitcast(fmt), scales=s[:], in_=src[:].rearrange("p n t -> p (n t)"))

        done = []

        def quant_once(f):
            if f not in done:
                done.append(f)
                quant_in(f)

        def d_lay(c, fg):
            t = grps.tile([P, W, 4], BF16, name="grp", align_bytes=64)
            dst = t[:].rearrange("p (c i) j -> p c j i", i=4)
            src = draw[c][:, :, fg * W:(fg + 1) * W].rearrange("p j (c i) -> p c j i", i=4)
            if (c, fg) in SCALAR_IL:
                nc.scalar.copy(out=dst, in_=src)
            else:
                nc.vector.tensor_copy(out=dst, in_=src)
            dg[c, fg] = t

        def d_quant(c, fg):
            a = keep.tile([P, W], U32, name="dc%d%d" % (c, fg), align_bytes=64)
            b = keep.tile([P, W], U8, name="ds%d%d" % (c, fg), align_bytes=64)
            nc.vector.quantize_mx(out=a[:].bitcast(E4M3), scales=b[:], in_=dg[c, fg][:].rearrange("p n t -> p (n t)"))
            dc[c, fg], ds[c, fg] = a, b

        def s1_pass(y, h, fg, s, c):
            nc.tensor.matmul_mx(
                out=y[:],
                lhsT=zc[c, h][:, s * P:(s + 1) * P].bitcast(E4M3),
                lhsT_scale=zs[c, h][:, s * P:(s + 1) * P],
                rhs=dc[c, fg][:].bitcast(E4M3),
                rhs_scale=ds[c, fg][:],
                start=(c == 0),
                stop=(c == CH - 1),
            )

        def residual(y, h, fg, s):
            if s == 0:
                ew[h, fg] = es.tile([P, 4, W], BF16, name="ew")
            r = vs.tile([P, W], F32, name="v")
            nc.vector.tensor_tensor(
                r[:].rearrange("p (u w e) -> p u w e", u=2, e=2),
                y[:].rearrange("p (w u e) -> p u w e", u=2, e=2),
                xraw[h][:, s, fg * W:(fg + 1) * W].rearrange("p (w u e) -> p u w e", u=2, e=2),
                ALU.subtract)
            weigh = nc.vector.tensor_tensor if (h, fg, s) in VECTOR_WEIGHS else nc.gpsimd.tensor_tensor
            weigh(ew[h, fg][:, s, :], r[:], prec_all[:, fg * W:(fg + 1) * W], ALU.mult)

        def s1_unit(h, fg, s):
            y = acc.tile([P, W], F32, name="sums")
            for c in range(CH):
                s1_pass(y, h, fg, s, c)
            residual(y, h, fg, s)

        leaf = {}
        pend = {}

        def s2_sums(g, h, j):
            y = acc.tile([P, W], F32, name="sums")
            for fg in range(FG):
                nc.tensor.matmul_mx(
                    out=y[:],
                    lhsT=tcod[g, fg][:, j * P:(j + 1) * P].bitcast(E4M3),
                    lhsT_scale=tsc[g, fg][:, j * P:(j + 1) * P],
                    rhs=ec[h, fg][:].bitcast(E5M2),
                    rhs_scale=esc[h, fg][:],
                    start=(fg == 0),
                    stop=(fg == FG - 1),
                )
            return y

        def col(name, g, j):
            return consts[name][:, g, j:j + 1]

        def gradient_step(y, g, h, j):
            v = vs.tile([P, W], F32, name="v")
            nc.vector.scalar_tensor_tensor(
                out=v[:], in0=y[:], scalar=col("neta", g, j), in1=zT["z", g, h][:, :, j], op0=ALU.mult, op1=ALU.add)
            pend[g, h, j] = v

        def split(g, h, j, kind):
            v = pend[g, h, j]
            if j % 2 == 0:
                t = bigs.tile([P, 2, 2, W], F32, name="big")
                leaf[g, h, j] = t[:, 0]
                leaf[g, h, j + 1] = t[:, 1]
            t = leaf[g, h, j]
            if kind == "E":
                nc.scalar.activation(t[:, 0, :], v[:], ACT.Relu, bias=col("nth", g, j))
                nc.scalar.activation(t[:, 0, :], t[:, 0, :], ACT.Identity, scale=col("gain", g, j), bias=col("hth", g, j))
            else:
                nc.vector.tensor_scalar(t[:, 0, :], v[:], col("th", g, j), col("gain", g, j), ALU.max, ALU.mult)
            nc.vector.tensor_scalar(t[:, 1, :], v[:], col("nth", g, j), col("gain", g, j), ALU.min, ALU.mult)

        def turn_out(g, h, s, engine):
            bank = turn.tile([P, 4, P], F32, name="bank")
            cols = slice(s * P, (s + 1) * P)
            for j in range(4):
                for k in range(2):
                    nc.tensor.matmul(bank[:, j, :], lhsT=leaf[g, h, j][:, k, cols], rhs=ident[:], is_transpose=True,
                                     start=(k == 0), stop=(k == 1))
            o = outs.tile([P, W], F32, name="o")
            src = bank[:].rearrange("p j n -> p n j")
            dst = o[:].rearrange("p (n j) -> p n j", j=4)
            if engine == "scalar":
                nc.scalar.copy(out=dst, in_=src)
            else:
                nc.vector.tensor_copy(out=dst, in_=src)
            r = h * W + s * P
            nc.sync.dma_start(out=out[r:r + P, g * W:(g + 1) * W], in_=o[:])

        order = [(g, h) for h in range(HALVES) for g in range(CH)]

        def group(n, between, after):
            g, h = order[n]
            for j in range(4):
                gradient_step(s2_sums(g, h, j), g, h, j)
                if j == 1:
                    between()
                if j >= LAG:
                    split(g, h, j - LAG, KINDS[n][j - LAG])
            for j in range(4 - LAG, 4):
                split(g, h, j, KINDS[n][j])
            after()

        for name in LOADS.split(" "):
            if name == "r":
                load_rows()
            elif name[0] == "z":
                load_z(int(name[1]), int(name[2]))
            elif name[0] == "x":
                load_x(int(name[1]))
            else:
                load_d(int(name[1]))

        first = []
        for s in range(4):
            y = acc.tile([P, W], F32, name="sums")
            first.append(y)
        warm_up(WARM0)
        make_consts()
        for c in range(CH):
            turn_in(("z", c, 0))
            warm_up(WARM[c])
            d_lay(c, 0)
            quant_in(("z", c, 0))
            d_quant(c, 0)
            d_lay(c, 1)
            if c == SPREAD:
                spread_prec()
            if c > 0:
                for s in range(4):
                    s1_pass(first[s], 0, 0, s, c - 1)
                for f in HEAD[c - 1]:
                    turn_in(f)
            d_quant(c, 1)
            if c > 1:
                for f in HEAD[c - 2]:
                    quant_in(f)

        def lay_ahead(fs):
            for f in fs:
                if f in WORDS or f in VECTOR_WORDS:
                    lay_words(f)

        lay_ahead(SLOTS[0])
        for s in range(4):
            s1_pass(first[s], 0, 0, s, 3)
            residual(first[s], 0, 0, s)
        for f in HEAD[2]:
            quant_in(f)
        for n in range(12):
            h, fg, s = ((0, 1), (1, 0), (1, 1))[n // 4] + (n % 4,)
            if n + 1 < 12:
                lay_ahead(SLOTS[n + 1])
            s1_unit(h, fg, s)
            for f in SLOTS[n]:
                turn_in(f)
            if n > 0:
                for f in SLOTS[n - 1]:
                    quant_once(f)
            if n == 3:
                for f in SLOTS[3]:
                    if f[0] == "z":
                        quant_once(f)
        for f in SLOTS[11]:
            quant_in(f)

        for n in range(8):
            def between(n=n):
                if SPLIT and n > 1:
                    for s in (2, 3):
                        turn_out(*order[n - 2], s, OUT[s])
                if n < len(AFTER):
                    for f in AFTER[n]:
                        turn_in(f)
                if 0 < n <= len(AFTER):
                    for f in AFTER[n - 1]:
                        quant_in(f)

            def after(n=n):
                if n > 0:
                    for s in (0, 1) if SPLIT else range(4):
                        turn_out(*order[n - 1], s, OUT[s])
            group(n, between, after)
        if SPLIT:
            for s in (2, 3):
                turn_out(*order[6], s, "scalar")
        for s in range(4):
            turn_out(*order[7], s, LAST[s])
